import numpy as np
import ml_dtypes


def mxq(x, axis, fmt="e4m3"):
    dtype, down = {"e4m3": (ml_dtypes.float8_e4m3fn, 7), "e5m2": (ml_dtypes.float8_e5m2, 14)}[fmt]
    v = np.moveaxis(np.asarray(x, np.float32).astype(ml_dtypes.bfloat16).astype(np.float64), axis, -1)
    blocks = v.reshape(v.shape[:-1] + (-1, 32))
    amax = np.abs(blocks).max(-1, keepdims=True)
    byte = np.maximum(np.where(amax > 0, np.frexp(amax)[1] - 1 + 127, 0) - down, 1)
    scale = np.exp2(byte - 127.0)
    codes = (blocks / scale).astype(np.float32).astype(dtype).astype(np.float64)
    return np.moveaxis((codes * scale).reshape(v.shape), -1, axis)


WIDE = False


def mx_kscale(k):
    if not WIDE:
        return np.ones(k)
    levels = np.array([10, -10, 5, -5, 0])
    if k % 512:
        return np.exp2(np.random.permutation(np.resize(levels, k // 32))).repeat(32)
    a = np.empty((k // 512, 16))
    for p in range(k // 512):
        a[p, :8] = np.random.permutation(np.resize(levels, 8))
        for g in range(8):
            far = levels[np.abs(levels - a[p, g]) >= 10]
            a[p, g + 8] = far[np.random.randint(len(far))]
    return np.exp2(a.ravel()).repeat(32)


def f64(x):
    return np.asarray(x).astype(np.float64)


def striped(idx):
    return np.tile(idx.reshape(-1, 16).T, (8, 1)).astype(np.uint16)


def unstriped(offs):
    return offs[:16].T.reshape(-1).astype(np.int64)


E2M1 = np.array([0.0, 0.5, 1.0, 1.5, 2.0, 3.0, 4.0, 6.0, -0.0, -0.5, -1.0, -1.5, -2.0, -3.0, -4.0, -6.0])


def pack_weight(w, fmt):
    k, n = w.shape
    w = f64(np.asarray(w, np.float32).astype(ml_dtypes.bfloat16)).reshape(k // 32, 32, n)
    amax = np.abs(w).max(1)
    if fmt == "e4m3":
        byte = np.frexp(amax)[1] - 1 + 127 - 7
    else:
        mant, ex = np.frexp(amax / 6.0)
        byte = np.where(mant > 0.5, ex, ex - 1) + 127
    byte = np.clip(np.where(amax > 0, byte, 1), 1, 254)
    scaled = (w * np.exp2(127.0 - byte)[:, None, :]).reshape(k, n).astype(np.float32)
    by_word = np.ascontiguousarray(scaled.reshape(k // 512, 128, 4, n).transpose(0, 1, 3, 2))
    if fmt == "e4m3":
        words = by_word.astype(ml_dtypes.float8_e4m3fn).view(np.uint8)
    else:
        c = by_word.astype(ml_dtypes.float4_e2m1fn).view(np.uint8) & 0xF
        words = (c[..., 0::2] | (c[..., 1::2] << 4)).reshape(k // 512, 128, 2 * n)
    return np.ascontiguousarray(words), np.ascontiguousarray(byte.astype(np.uint8).reshape(k // 512, 16, n))


def unpack_weight(words, scales, fmt):
    g, _, n = scales.shape
    words = np.ascontiguousarray(words).reshape(g, 128, n, -1)
    if fmt == "e4m3":
        vals = words.view(ml_dtypes.float8_e4m3fn).astype(np.float64)
    else:
        nib = np.empty((g, 128, n, 4), np.uint8)
        nib[..., 0::2] = words & 0xF
        nib[..., 1::2] = words >> 4
        vals = E2M1[nib]
    vals = vals * np.repeat(np.exp2(scales.astype(np.float64) - 127.0), 8, axis=1)[..., None]
    return vals.transpose(0, 1, 3, 2).reshape(g * 512, n)


def gelu(v):
    return 0.5 * v * (1.0 + np.tanh(np.sqrt(2.0 / np.pi) * (v + 0.044715 * v**3)))


K, H, N, T, S = 1024, 512, 640, 4096, 1024

def setup_inputs():
    n = np.random.standard_normal
    s = mx_kscale(K)[:, None]
    u = mx_kscale(H)[:, None]
    tab_words, tab_scales = pack_weight(n((K, T)) * s, "e2m1")
    offs = striped(np.random.permutation(T)[:S])
    offs2 = striped(np.random.permutation(T)[:S])
    wv = (n((K, H)) / np.sqrt(K) / s * u.T).astype(np.float32)
    wo_words, wo_scales = pack_weight(n((K, H)) / np.sqrt(K) / s * u.T, "e4m3")
    bv = (0.5 * n(H) * u[:, 0]).astype(np.float32)
    bo = (0.5 * n(H) * u[:, 0]).astype(np.float32)
    ws_words, ws_scales = pack_weight(0.7 * n((H, N)) / np.sqrt(H) / u, "e2m1")
    wd = (0.7 * n((H, N)) / np.sqrt(H) / u).astype(np.float32)
    return {"tab_words": tab_words, "tab_scales": tab_scales, "offs": offs, "offs2": offs2,
            "wv": wv, "wo_words": wo_words, "wo_scales": wo_scales, "bv": bv, "bo": bo,
            "ws_words": ws_words, "ws_scales": ws_scales, "wd": wd}

def reference(tab_words, tab_scales, offs, offs2, wv, wo_words, wo_scales, bv, bo, ws_words, ws_scales, wd):
    TW = unpack_weight(tab_words, tab_scales, "e2m1")
    v = TW[:, unstriped(offs)]
    v2 = TW[:, unstriped(offs2)]
    wo = unpack_weight(wo_words, wo_scales, "e4m3")
    ws = unpack_weight(ws_words, ws_scales, "e2m1")
    p = (mxq(f64(wv), 0, "e4m3").T @ v) + f64(bv)[:, None]
    q = (wo.T @ v2) + f64(bo)[:, None]
    a = mxq(p + q, 0, "e4m3")
    d = mxq(p - q, 0, "e4m3")
    y1 = ws.T @ a
    y2 = mxq(f64(wd), 0, "e4m3").T @ d
    return y1 * y2

@@ -1,0 +1,248 @@
+from contextlib import ExitStack
+
+import concourse.mybir as mybir
+
+K, H, N, T, S = 1024, 512, 640, 4096, 1024
+FLOPS = 2 * S * (2 * K * H + 2 * H * N)
+
+F32 = mybir.dt.float32
+BF16 = mybir.dt.bfloat16
+I32 = mybir.dt.int32
+U32 = mybir.dt.uint32
+U16 = mybir.dt.uint16
+U8 = mybir.dt.uint8
+FP8X4 = mybir.dt.float8_e4m3fn_x4
+FP4X4 = mybir.dt.float4_e2m1fn_x4
+IDENTITY = mybir.ActivationFunctionType.Identity
+ADD = mybir.AluOpType.add
+SUBTRACT = mybir.AluOpType.subtract
+MULT = mybir.AluOpType.mult
+
+P = 128
+PACK = 4
+K_PASS = P * PACK
+PASSES = K // K_PASS
+CHUNK = 512
+CHUNKS = S // CHUNK
+N_TILES = N // P
+QUADS = 4
+SHIFT = 16
+HALF = H // 2
+PART = CHUNK // 2
+
+
+def tile_list_metaphor_spotting_kernel(
+    tc, tab_words, tab_scales, offs, offs2, wv, wo_words, wo_scales, bv, bo, ws_words, ws_scales, wd, out
+):
+    nc = tc.nc
+    with ExitStack() as ctx:
+        keep = ctx.enter_context(tc.tile_pool(name="keep", bufs=1))
+        work = ctx.enter_context(tc.tile_pool(name="work", bufs=2))
+        psum = ctx.enter_context(tc.psum_pool(name="psum", bufs=8))
+
+        table_scales = keep.tile([P, T], U8, name="table_scales", align_bytes=64)
+        nc.vector.memset(table_scales[:].bitcast(I32), 0)
+        wo_scales_raw = keep.tile([P, PASSES * H], U8, name="wo_scales_raw", align_bytes=64)
+        nc.vector.memset(wo_scales_raw[:].bitcast(I32), 0)
+        ws_plane = keep.tile([P, N], U8, name="ws_plane", align_bytes=64)
+        nc.vector.memset(ws_plane[:].bitcast(I32), 0)
+        moved = []
+        for side in range(2):
+            tile = keep.tile([P, S], U8, name=f"moved{side}", align_bytes=64)
+            nc.vector.memset(tile[:].bitcast(I32), 0)
+            moved.append(tile)
+
+        table_words = [keep.tile([P, T], U16, name=f"table_words{a}", align_bytes=64) for a in range(PASSES)]
+        nc.sync.dma_start(out=table_words[0][:].bitcast(I32), in_=tab_words[0].bitcast(I32))
+        scale_rows = tab_scales.rearrange("a (q r) t -> r q a t", r=4)
+        for r in range(4):
+            nc.sync.dma_start(out=table_scales[r:P:SHIFT, :].bitcast(I32), in_=scale_rows[r].bitcast(I32))
+        lists = []
+        for side, src in enumerate((offs2, offs)):
+            tile = keep.tile([P, S // 16], U16, name=f"list{side}")
+            nc.sync.dma_start(tile[:], src)
+            lists.append(tile)
+        wo_raw = keep.tile([P, PASSES, H], I32, name="wo_raw", align_bytes=64)
+        nc.sync.dma_start(out=wo_raw[:], in_=wo_words.rearrange("a p c i -> p a (c i)").bitcast(I32))
+        for q in range(QUADS):
+            nc.gpsimd.dma_start(
+                out=wo_scales_raw[32 * q : 32 * q + 4, :].bitcast(I32).rearrange("r (a c) -> r a c", a=PASSES),
+                in_=wo_scales[:, 4 * q : 4 * q + 4, :].rearrange("a r c -> r a c").bitcast(I32),
+            )
+        wv_raw = {}
+        for a in range(PASSES):
+            for h in range(2):
+                tile = keep.tile([P, PACK, HALF], F32, name=f"wv_raw{a}{h}")
+                rows = wv[a * K_PASS : (a + 1) * K_PASS, h * HALF : (h + 1) * HALF]
+                nc.sync.dma_start(out=tile[:], in_=rows.rearrange("(p j) c -> p j c", j=PACK))
+                wv_raw[a, h] = tile
+        nc.sync.dma_start(out=table_words[1][:].bitcast(I32), in_=tab_words[1].bitcast(I32))
+        biases = []
+        for side, src in enumerate((bo, bv)):
+            tile = keep.tile([P, PACK], F32, name=f"bias{side}")
+            nc.sync.dma_start(out=tile[:], in_=src.rearrange("(p t) -> p t", t=PACK))
+            biases.append(tile)
+
+        picked_scales = []
+        for side in range(2):
+            tile = keep.tile([P, S], U8, name=f"picked_scales{side}", align_bytes=64)
+            nc.vector.tensor_copy(tile[:], table_scales[:].indirect(lists[side][:]))
+            nc.sync.dma_start(out=moved[side][0 : P - SHIFT, :].bitcast(I32), in_=tile[SHIFT:P, :].bitcast(I32))
+            picked_scales.append((tile, moved[side]))
+
+        wd_raw = keep.tile([P, PACK, N], F32, name="wd_raw")
+        nc.sync.dma_start(out=wd_raw[:], in_=wd.rearrange("(p j) n -> p j n", j=PACK))
+        ws_codes = keep.tile([P, 2 * N], U8, name="ws_codes", align_bytes=64)
+        nc.sync.dma_start(out=ws_codes[:].bitcast(I32), in_=ws_words[0].bitcast(I32))
+
+        wo_codes = keep.tile([P, PASSES, H], I32, name="wo_codes", align_bytes=64)
+        nc.gpsimd.tensor_copy(
+            out=wo_codes[:].rearrange("p a (t m) -> p a t m", t=PACK),
+            in_=wo_raw[:].rearrange("p a (m t) -> p a t m", t=PACK),
+        )
+        wo_plane = keep.tile([P, PASSES, H], U8, name="wo_plane", align_bytes=64)
+        nc.gpsimd.tensor_copy(
+            out=wo_plane[:].rearrange("p a (t m) -> p a t m", t=PACK),
+            in_=wo_scales_raw[:].rearrange("p (a m t) -> p a t m", a=PASSES, t=PACK),
+        )
+
+        for q in range(QUADS):
+            nc.gpsimd.dma_start(
+                out=ws_plane[32 * q : 32 * q + 4, :].bitcast(I32), in_=ws_scales[0, 4 * q : 4 * q + 4, :].bitcast(I32)
+            )
+
+        picked = {}
+
+        def gather_words(side, a, c):
+            tile = keep.tile([P, CHUNK], U16, name=f"picked{side}{a}{c}", align_bytes=64)
+            cols = CHUNK // 16
+            nc.vector.tensor_copy(tile[:], table_words[a][:].indirect(lists[side][:, c * cols : (c + 1) * cols]))
+            picked[side, a, c] = tile
+
+        for c in range(CHUNKS):
+            for side in range(2):
+                gather_words(side, 0, c)
+
+        wv_codes = keep.tile([P, PASSES, H], U32, name="wv_codes", align_bytes=64)
+        wv_plane = keep.tile([P, PASSES, H], U8, name="wv_plane", align_bytes=64)
+        for a in range(PASSES):
+            grouped = keep.tile([P, PACK, P, PACK], BF16, name=f"wv_grouped{a}", align_bytes=64)
+            for h in range(2):
+                nc.scalar.copy(
+                    out=grouped[:, :, h * (P // 2) : (h + 1) * (P // 2), :].rearrange("p t m j -> p m j t"),
+                    in_=wv_raw[a, h][:].rearrange("p j (m t) -> p m j t", t=PACK),
+                )
+            nc.vector.quantize_mx(
+                out=wv_codes[:, a, :].bitcast(FP8X4),
+                scales=wv_plane[:, a, :],
+                in_=grouped[:].rearrange("p t m j -> p (t m j)"),
+            )
+
+        weights = ((wo_codes, wo_plane), (wv_codes, wv_plane))
+        projected = {}
+
+        def first_stage(c):
+            cols = slice(c * CHUNK, (c + 1) * CHUNK)
+            banks = {}
+            for a in range(PASSES):
+                for side in range(2):
+                    if a == 1:
+                        gather_words(side, 1, c)
+                    codes, plane = weights[side]
+                    for t in range(PACK):
+                        if a == 0:
+                            banks[side, t] = psum.tile([P, CHUNK], F32, name="bank")
+                        nc.tensor.matmul_mx(
+                            out=banks[side, t][:],
+                            lhsT=codes[:, a, t * P : (t + 1) * P].bitcast(FP8X4),
+                            lhsT_scale=plane[:, a, t * P : (t + 1) * P],
+                            rhs=picked[side, a, c][:].bitcast(FP4X4),
+                            rhs_scale=picked_scales[side][a][:, cols],
+                            start=(a == 0),
+                            stop=(a == PASSES - 1),
+                        )
+            for h in range(2):
+                for side in range(2):
+                    tile = work.tile([P, PACK, PART], F32, name=f"projected{side}", bufs=4)
+                    for t in range(PACK):
+                        nc.scalar.activation(
+                            out=tile[:, t, :],
+                            in_=banks[side, t][:, h * PART : (h + 1) * PART],
+                            func=IDENTITY,
+                            bias=biases[side][:, t : t + 1],
+                        )
+                    projected[side, c, h] = tile
+
+        mixed = {}
+
+        def mix(c):
+            grouped = [work.tile([P, CHUNK, PACK], BF16, name=f"mixed{which}", align_bytes=64) for which in range(2)]
+            for h in range(2):
+                q_in = projected[0, c, h][:].rearrange("p t (g i) -> p g t i", i=4)
+                p_in = projected[1, c, h][:].rearrange("p t (g i) -> p g t i", i=4)
+                for which, op in enumerate((ADD, SUBTRACT)):
+                    part = grouped[which][:, h * PART : (h + 1) * PART, :]
+                    nc.vector.tensor_tensor(out=part.rearrange("p (g i) t -> p g t i", i=4), in0=p_in, in1=q_in, op=op)
+            for which in range(2):
+                codes = work.tile([P, CHUNK], U32, name=f"mixed_codes{which}", align_bytes=64)
+                plane = work.tile([P, CHUNK], U8, name=f"mixed_plane{which}", align_bytes=64)
+                nc.vector.quantize_mx(
+                    out=codes[:].bitcast(FP8X4), scales=plane[:], in_=grouped[which][:].rearrange("p j t -> p (j t)")
+                )
+                mixed[which, c] = (codes, plane)
+
+        for c in range(CHUNKS):
+            first_stage(c)
+
+        wd_grouped = keep.tile([P, N, PACK], BF16, name="wd_grouped", align_bytes=64)
+        nc.gpsimd.tensor_scalar(
+            out=wd_grouped[:].rearrange("p (g i) j -> p g j i", i=4),
+            in0=wd_raw[:].rearrange("p j (g i) -> p g j i", i=4),
+            scalar1=1.0,
+            scalar2=0.0,
+            op0=MULT,
+            op1=ADD,
+        )
+        wd_codes = keep.tile([P, N], U32, name="wd_codes", align_bytes=64)
+        wd_plane = keep.tile([P, N], U8, name="wd_plane", align_bytes=64)
+        for lo, hi in ((0, 512), (512, N)):
+            nc.vector.quantize_mx(
+                out=wd_codes[:, lo:hi].bitcast(FP8X4),
+                scales=wd_plane[:, lo:hi],
+                in_=wd_grouped[:, lo:hi, :].rearrange("p n j -> p (n j)"),
+            )
+
+        def second_stage(c):
+            (a_codes, a_plane), (d_codes, d_plane) = mixed[0, c], mixed[1, c]
+            for n in range(N_TILES):
+                rows = slice(n * P, (n + 1) * P)
+                y1 = psum.tile([P, CHUNK], F32, name="bank")
+                nc.tensor.matmul_mx(
+                    out=y1[:],
+                    lhsT=ws_codes[:, 2 * n * P : 2 * (n + 1) * P].bitcast(FP4X4),
+                    lhsT_scale=ws_plane[:, rows],
+                    rhs=a_codes[:].bitcast(FP8X4),
+                    rhs_scale=a_plane[:],
+                    start=True,
+                    stop=True,
+                )
+                y2 = psum.tile([P, CHUNK], F32, name="bank")
+                nc.tensor.matmul_mx(
+                    out=y2[:],
+                    lhsT=wd_codes[:, rows].bitcast(FP8X4),
+                    lhsT_scale=wd_plane[:, rows],
+                    rhs=d_codes[:].bitcast(FP8X4),
+                    rhs_scale=d_plane[:],
+                    start=True,
+                    stop=True,
+                )
+                y1_sb = work.tile([P, CHUNK], F32, name="y1_sb", bufs=4)
+                nc.scalar.copy(out=y1_sb[:], in_=y1[:])
+                result = work.tile([P, CHUNK], F32, name="result", bufs=10)
+                nc.vector.tensor_tensor(out=result[:], in0=y2[:], in1=y1_sb[:], op=MULT)
+                nc.sync.dma_start(out=out[rows, c * CHUNK : (c + 1) * CHUNK], in_=result[:])
+
+        for c in range(CHUNKS):
+            mix(c)
+        for c in range(CHUNKS):
+            second_stage(c)

@@ -37,172 +37,119 @@ def tile_list_metaphor_spotting_kernel(
     nc = tc.nc
     with ExitStack() as ctx:
         keep = ctx.enter_context(tc.tile_pool(name="keep", bufs=1))
-        work = ctx.enter_context(tc.tile_pool(name="work", bufs=2))
-        psum = ctx.enter_context(tc.psum_pool(name="psum", bufs=8))
+        work = ctx.enter_context(tc.tile_pool(name="work", bufs=1))
+        psum = ctx.enter_context(tc.psum_pool(name="psum", bufs=1))
+
+        def bank(index, shape):
+            return psum.tile(shape, F32, name=f"bank{index}", tag=f"bank{index}")
 
         table_scales = keep.tile([P, T], U8, name="table_scales", align_bytes=64)
         nc.vector.memset(table_scales[:].bitcast(I32), 0)
         wo_scales_raw = keep.tile([P, PASSES * H], U8, name="wo_scales_raw", align_bytes=64)
         nc.vector.memset(wo_scales_raw[:].bitcast(I32), 0)
+        moved = keep.tile([P, 2 * S], U8, name="moved", align_bytes=64)
+        nc.vector.memset(moved[:].bitcast(I32), 0)
         ws_plane = keep.tile([P, N], U8, name="ws_plane", align_bytes=64)
         nc.vector.memset(ws_plane[:].bitcast(I32), 0)
-        moved = []
-        for side in range(2):
-            tile = keep.tile([P, S], U8, name=f"moved{side}", align_bytes=64)
-            nc.vector.memset(tile[:].bitcast(I32), 0)
-            moved.append(tile)
 
+        lists = [keep.tile([P, S // 16], U16, name=f"list{side}") for side in range(2)]
         table_words = [keep.tile([P, T], U16, name=f"table_words{a}", align_bytes=64) for a in range(PASSES)]
+        nc.sync.dma_start(lists[0][:], offs2)
         nc.sync.dma_start(out=table_words[0][:].bitcast(I32), in_=tab_words[0].bitcast(I32))
         scale_rows = tab_scales.rearrange("a (q r) t -> r q a t", r=4)
         for r in range(4):
             nc.sync.dma_start(out=table_scales[r:P:SHIFT, :].bitcast(I32), in_=scale_rows[r].bitcast(I32))
-        lists = []
-        for side, src in enumerate((offs2, offs)):
-            tile = keep.tile([P, S // 16], U16, name=f"list{side}")
-            nc.sync.dma_start(tile[:], src)
-            lists.append(tile)
+        nc.sync.dma_start(lists[1][:], offs)
         wo_raw = keep.tile([P, PASSES, H], I32, name="wo_raw", align_bytes=64)
         nc.sync.dma_start(out=wo_raw[:], in_=wo_words.rearrange("a p c i -> p a (c i)").bitcast(I32))
-        for q in range(QUADS):
-            nc.gpsimd.dma_start(
-                out=wo_scales_raw[32 * q : 32 * q + 4, :].bitcast(I32).rearrange("r (a c) -> r a c", a=PASSES),
-                in_=wo_scales[:, 4 * q : 4 * q + 4, :].rearrange("a r c -> r a c").bitcast(I32),
+        wo_rows = wo_scales.rearrange("a (q r) c -> r q a c", r=4)
+        for r in range(4):
+            nc.sync.dma_start(
+                out=wo_scales_raw[r:P:32, :].bitcast(I32).rearrange("q (a c) -> q a c", a=PASSES),
+                in_=wo_rows[r].bitcast(I32),
             )
-        wv_raw = {}
+        wv_raw = []
         for a in range(PASSES):
-            for h in range(2):
-                tile = keep.tile([P, PACK, HALF], F32, name=f"wv_raw{a}{h}")
-                rows = wv[a * K_PASS : (a + 1) * K_PASS, h * HALF : (h + 1) * HALF]
-                nc.sync.dma_start(out=tile[:], in_=rows.rearrange("(p j) c -> p j c", j=PACK))
-                wv_raw[a, h] = tile
+            tile = keep.tile([P, PACK, H], F32, name=f"wv_raw{a}")
+            rows = wv[a * K_PASS : (a + 1) * K_PASS, :]
+            nc.sync.dma_start(out=tile[:], in_=rows.rearrange("(p j) c -> p j c", j=PACK))
+            wv_raw.append(tile)
         nc.sync.dma_start(out=table_words[1][:].bitcast(I32), in_=tab_words[1].bitcast(I32))
+
+        picked = {}
+        picked_scales = keep.tile([P, 2 * S], U8, name="picked_scales", align_bytes=64)
+
+        def gather_first(side):
+            tile = keep.tile([P, S], U16, name=f"picked{side}0", align_bytes=64)
+            nc.vector.tensor_copy(tile[:], table_words[0][:].indirect(lists[side][:]))
+            for c in range(CHUNKS):
+                picked[side, 0, c] = tile[:, c * CHUNK : (c + 1) * CHUNK]
+
+        gather_first(0)
+        for side in range(2):
+            nc.vector.tensor_copy(picked_scales[:, side * S : (side + 1) * S], table_scales[:].indirect(lists[side][:]))
+        gather_first(1)
+        nc.sync.dma_start(out=moved[0 : P - SHIFT, :].bitcast(I32), in_=picked_scales[SHIFT:P, :].bitcast(I32))
+        table_planes = (picked_scales, moved)
+
+        wd_raw = []
+        for h in range(2):
+            tile = work.tile([P, PACK, N // 2], F32, name=f"wd_raw{h}", tag=f"wd_raw{h}")
+            cols = wd[:, h * (N // 2) : (h + 1) * (N // 2)]
+            nc.sync.dma_start(out=tile[:], in_=cols.rearrange("(p j) n -> p j n", j=PACK))
+            wd_raw.append(tile)
         biases = []
         for side, src in enumerate((bo, bv)):
             tile = keep.tile([P, PACK], F32, name=f"bias{side}")
             nc.sync.dma_start(out=tile[:], in_=src.rearrange("(p t) -> p t", t=PACK))
             biases.append(tile)
-
-        picked_scales = []
-        for side in range(2):
-            tile = keep.tile([P, S], U8, name=f"picked_scales{side}", align_bytes=64)
-            nc.vector.tensor_copy(tile[:], table_scales[:].indirect(lists[side][:]))
-            nc.sync.dma_start(out=moved[side][0 : P - SHIFT, :].bitcast(I32), in_=tile[SHIFT:P, :].bitcast(I32))
-            picked_scales.append((tile, moved[side]))
-
-        wd_raw = keep.tile([P, PACK, N], F32, name="wd_raw")
-        nc.sync.dma_start(out=wd_raw[:], in_=wd.rearrange("(p j) n -> p j n", j=PACK))
         ws_codes = keep.tile([P, 2 * N], U8, name="ws_codes", align_bytes=64)
         nc.sync.dma_start(out=ws_codes[:].bitcast(I32), in_=ws_words[0].bitcast(I32))
+        ws_rows = ws_scales[0].rearrange("(q r) n -> r q n", r=4)
+        for r in range(4):
+            nc.sync.dma_start(out=ws_plane[r:P:32, :].bitcast(I32), in_=ws_rows[r].bitcast(I32))
 
         wo_codes = keep.tile([P, PASSES, H], I32, name="wo_codes", align_bytes=64)
-        nc.gpsimd.tensor_copy(
-            out=wo_codes[:].rearrange("p a (t m) -> p a t m", t=PACK),
-            in_=wo_raw[:].rearrange("p a (m t) -> p a t m", t=PACK),
+        nc.vector.tensor_copy(
+            out=wo_codes[:].rearrange("p a (t g i) -> p a g t i", t=PACK, i=4),
+            in_=wo_raw[:].rearrange("p a (g i t) -> p a g t i", t=PACK, i=4),
         )
         wo_plane = keep.tile([P, PASSES, H], U8, name="wo_plane", align_bytes=64)
-        nc.gpsimd.tensor_copy(
-            out=wo_plane[:].rearrange("p a (t m) -> p a t m", t=PACK),
-            in_=wo_scales_raw[:].rearrange("p (a m t) -> p a t m", a=PASSES, t=PACK),
+        nc.vector.tensor_copy(
+            out=wo_plane[:].rearrange("p a (t g i) -> p a g t i", t=PACK, i=16),
+            in_=wo_scales_raw[:].rearrange("p (a g i t) -> p a g t i", a=PASSES, t=PACK, i=16),
         )
 
-        for q in range(QUADS):
-            nc.gpsimd.dma_start(
-                out=ws_plane[32 * q : 32 * q + 4, :].bitcast(I32), in_=ws_scales[0, 4 * q : 4 * q + 4, :].bitcast(I32)
+        wv_codes, wv_plane = [], []
+        for a in range(PASSES):
+            grouped = work.tile([P, PACK, P, PACK], BF16, name=f"wv_grouped{a}", tag=f"wv_grouped{a}", align_bytes=64)
+            nc.scalar.copy(
+                out=grouped[:].rearrange("p t m j -> p m j t"),
+                in_=wv_raw[a][:].rearrange("p j (m t) -> p m j t", t=PACK),
             )
+            codes = keep.tile([P, H], U32, name=f"wv_codes{a}", align_bytes=64)
+            plane = keep.tile([P, H], U8, name=f"wv_plane{a}", align_bytes=64)
+            nc.vector.quantize_mx(
+                out=codes[:].bitcast(FP8X4), scales=plane[:], in_=grouped[:].rearrange("p t m j -> p (t m j)")
+            )
+            wv_codes.append(codes)
+            wv_plane.append(plane)
 
-        picked = {}
-
-        def gather_words(side, a, c):
-            tile = keep.tile([P, CHUNK], U16, name=f"picked{side}{a}{c}", align_bytes=64)
-            cols = CHUNK // 16
-            nc.vector.tensor_copy(tile[:], table_words[a][:].indirect(lists[side][:, c * cols : (c + 1) * cols]))
-            picked[side, a, c] = tile
-
+        second = work.tile([P, 2 * S], U16, name="picked_second", tag="wv_grouped1", align_bytes=64)
         for c in range(CHUNKS):
             for side in range(2):
-                gather_words(side, 0, c)
-
-        wv_codes = keep.tile([P, PASSES, H], U32, name="wv_codes", align_bytes=64)
-        wv_plane = keep.tile([P, PASSES, H], U8, name="wv_plane", align_bytes=64)
-        for a in range(PASSES):
-            grouped = keep.tile([P, PACK, P, PACK], BF16, name=f"wv_grouped{a}", align_bytes=64)
-            for h in range(2):
-                nc.scalar.copy(
-                    out=grouped[:, :, h * (P // 2) : (h + 1) * (P // 2), :].rearrange("p t m j -> p m j t"),
-                    in_=wv_raw[a, h][:].rearrange("p j (m t) -> p m j t", t=PACK),
-                )
-            nc.vector.quantize_mx(
-                out=wv_codes[:, a, :].bitcast(FP8X4),
-                scales=wv_plane[:, a, :],
-                in_=grouped[:].rearrange("p t m j -> p (t m j)"),
-            )
-
-        weights = ((wo_codes, wo_plane), (wv_codes, wv_plane))
-        projected = {}
-
-        def first_stage(c):
-            cols = slice(c * CHUNK, (c + 1) * CHUNK)
-            banks = {}
-            for a in range(PASSES):
-                for side in range(2):
-                    if a == 1:
-                        gather_words(side, 1, c)
-                    codes, plane = weights[side]
-                    for t in range(PACK):
-                        if a == 0:
-                            banks[side, t] = psum.tile([P, CHUNK], F32, name="bank")
-                        nc.tensor.matmul_mx(
-                            out=banks[side, t][:],
-                            lhsT=codes[:, a, t * P : (t + 1) * P].bitcast(FP8X4),
-                            lhsT_scale=plane[:, a, t * P : (t + 1) * P],
-                            rhs=picked[side, a, c][:].bitcast(FP4X4),
-                            rhs_scale=picked_scales[side][a][:, cols],
-                            start=(a == 0),
-                            stop=(a == PASSES - 1),
-                        )
-            for h in range(2):
-                for side in range(2):
-                    tile = work.tile([P, PACK, PART], F32, name=f"projected{side}", bufs=4)
-                    for t in range(PACK):
-                        nc.scalar.activation(
-                            out=tile[:, t, :],
-                            in_=banks[side, t][:, h * PART : (h + 1) * PART],
-                            func=IDENTITY,
-                            bias=biases[side][:, t : t + 1],
-                        )
-                    projected[side, c, h] = tile
-
-        mixed = {}
-
-        def mix(c):
-            grouped = [work.tile([P, CHUNK, PACK], BF16, name=f"mixed{which}", align_bytes=64) for which in range(2)]
-            for h in range(2):
-                q_in = projected[0, c, h][:].rearrange("p t (g i) -> p g t i", i=4)
-                p_in = projected[1, c, h][:].rearrange("p t (g i) -> p g t i", i=4)
-                for which, op in enumerate((ADD, SUBTRACT)):
-                    part = grouped[which][:, h * PART : (h + 1) * PART, :]
-                    nc.vector.tensor_tensor(out=part.rearrange("p (g i) t -> p g t i", i=4), in0=p_in, in1=q_in, op=op)
-            for which in range(2):
-                codes = work.tile([P, CHUNK], U32, name=f"mixed_codes{which}", align_bytes=64)
-                plane = work.tile([P, CHUNK], U8, name=f"mixed_plane{which}", align_bytes=64)
-                nc.vector.quantize_mx(
-                    out=codes[:].bitcast(FP8X4), scales=plane[:], in_=grouped[which][:].rearrange("p j t -> p (j t)")
-                )
-                mixed[which, c] = (codes, plane)
-
-        for c in range(CHUNKS):
-            first_stage(c)
+                part = second[:, (2 * c + side) * CHUNK : (2 * c + side + 1) * CHUNK]
+                cols = CHUNK // 16
+                nc.vector.tensor_copy(part, table_words[1][:].indirect(lists[side][:, c * cols : (c + 1) * cols]))
+                picked[side, 1, c] = part
 
         wd_grouped = keep.tile([P, N, PACK], BF16, name="wd_grouped", align_bytes=64)
-        nc.gpsimd.tensor_scalar(
-            out=wd_grouped[:].rearrange("p (g i) j -> p g j i", i=4),
-            in0=wd_raw[:].rearrange("p j (g i) -> p g j i", i=4),
-            scalar1=1.0,
-            scalar2=0.0,
-            op0=MULT,
-            op1=ADD,
-        )
+        for h in range(2):
+            part = wd_grouped[:, h * (N // 2) : (h + 1) * (N // 2), :]
+            nc.scalar.copy(
+                out=part.rearrange("p (g i) j -> p g j i", i=4),
+                in_=wd_raw[h][:].rearrange("p j (g i) -> p g j i", i=4),
+            )
         wd_codes = keep.tile([P, N], U32, name="wd_codes", align_bytes=64)
         wd_plane = keep.tile([P, N], U8, name="wd_plane", align_bytes=64)
         for lo, hi in ((0, 512), (512, N)):
@@ -212,37 +159,142 @@ def tile_list_metaphor_spotting_kernel(
                 in_=wd_grouped[:, lo:hi, :].rearrange("p n j -> p (n j)"),
             )
 
-        def second_stage(c):
-            (a_codes, a_plane), (d_codes, d_plane) = mixed[0, c], mixed[1, c]
-            for n in range(N_TILES):
-                rows = slice(n * P, (n + 1) * P)
-                y1 = psum.tile([P, CHUNK], F32, name="bank")
-                nc.tensor.matmul_mx(
-                    out=y1[:],
-                    lhsT=ws_codes[:, 2 * n * P : 2 * (n + 1) * P].bitcast(FP4X4),
-                    lhsT_scale=ws_plane[:, rows],
-                    rhs=a_codes[:].bitcast(FP8X4),
-                    rhs_scale=a_plane[:],
-                    start=True,
-                    stop=True,
-                )
-                y2 = psum.tile([P, CHUNK], F32, name="bank")
-                nc.tensor.matmul_mx(
-                    out=y2[:],
-                    lhsT=wd_codes[:, rows].bitcast(FP8X4),
-                    lhsT_scale=wd_plane[:, rows],
-                    rhs=d_codes[:].bitcast(FP8X4),
-                    rhs_scale=d_plane[:],
-                    start=True,
-                    stop=True,
-                )
-                y1_sb = work.tile([P, CHUNK], F32, name="y1_sb", bufs=4)
-                nc.scalar.copy(out=y1_sb[:], in_=y1[:])
-                result = work.tile([P, CHUNK], F32, name="result", bufs=10)
-                nc.vector.tensor_tensor(out=result[:], in0=y2[:], in1=y1_sb[:], op=MULT)
-                nc.sync.dma_start(out=out[rows, c * CHUNK : (c + 1) * CHUNK], in_=result[:])
+        def weights(side, a, t):
+            cols = slice(t * P, (t + 1) * P)
+            if side == 0:
+                return wo_codes[:, a, cols], wo_plane[:, a, cols]
+            return wv_codes[a][:, cols], wv_plane[a][:, cols]
 
-        for c in range(CHUNKS):
-            mix(c)
-        for c in range(CHUNKS):
-            second_stage(c)
+        def first_pass(acc, side, a, t, c):
+            codes, plane = weights(side, a, t)
+            nc.tensor.matmul_mx(
+                out=acc[:],
+                lhsT=codes.bitcast(FP8X4),
+                lhsT_scale=plane,
+                rhs=picked[side, a, c].bitcast(FP4X4),
+                rhs_scale=table_planes[a][:, side * S + c * CHUNK : side * S + (c + 1) * CHUNK],
+                start=(a == 0),
+                stop=(a == PASSES - 1),
+            )
+
+        projected = {}
+
+        def empty(accs, side, c, lo, hi, tag):
+            tile = work.tile([P, PACK, hi - lo], F32, name=f"projected{side}{c}{lo}", tag=tag)
+            for t in range(PACK):
+                nc.scalar.activation(
+                    out=tile[:, t, :], in_=accs[side, t][:, lo:hi], func=IDENTITY, bias=biases[side][:, t : t + 1]
+                )
+            for h in range(lo // PART, hi // PART):
+                projected[side, 2 * c + h] = tile[:, :, h * PART - lo : (h + 1) * PART - lo]
+
+        def mix(unit, grouped):
+            q_in = projected[0, unit].rearrange("p t (g i) -> p g t i", i=4)
+            p_in = projected[1, unit].rearrange("p t (g i) -> p g t i", i=4)
+            for which, op in enumerate((ADD, SUBTRACT)):
+                nc.vector.tensor_tensor(
+                    out=grouped[which].rearrange("p (g i) t -> p g t i", i=4), in0=p_in, in1=q_in, op=op
+                )
+
+        def quantise(name, grouped, width):
+            codes = work.tile([P, width], U32, name=f"{name}_codes", align_bytes=64)
+            plane = work.tile([P, width], U8, name=f"{name}_plane", align_bytes=64)
+            nc.vector.quantize_mx(out=codes[:].bitcast(FP8X4), scales=plane[:], in_=grouped.rearrange("p j t -> p (j t)"))
+            return codes, plane
+
+        def second_pass(acc, which, n, operand):
+            rows = slice(n * P, (n + 1) * P)
+            if which == 0:
+                lhs, lhs_plane = ws_codes[:, 2 * n * P : 2 * (n + 1) * P].bitcast(FP4X4), ws_plane[:, rows]
+            else:
+                lhs, lhs_plane = wd_codes[:, rows].bitcast(FP8X4), wd_plane[:, rows]
+            nc.tensor.matmul_mx(
+                out=acc, lhsT=lhs, lhsT_scale=lhs_plane, rhs=operand[0][:].bitcast(FP8X4), rhs_scale=operand[1][:],
+                start=True, stop=True,
+            )
+
+        def copy_out(name, y1, shape):
+            tile = work.tile(shape, F32, name=f"y1_{name}")
+            nc.scalar.copy(out=tile[:], in_=y1)
+            return tile
+
+        def multiply(name, y1_sb, y2, shape, dest):
+            result = work.tile(shape, F32, name=f"result_{name}")
+            nc.vector.tensor_tensor(out=result[:], in0=y2, in1=y1_sb[:], op=MULT)
+            nc.sync.dma_start(out=dest, in_=result[:])
+
+        accs = {}
+        for a in range(PASSES):
+            for side in range(2):
+                for t in range(PACK):
+                    if a == 0:
+                        accs[side, t] = bank(PACK * side + t, [P, CHUNK])
+                    first_pass(accs[side, t], side, a, t, 0)
+        empty(accs, 0, 0, 0, PART, "wd_raw1")
+        empty(accs, 1, 0, 0, PART, "p0")
+        empty(accs, 0, 0, PART, CHUNK, "q1")
+        empty(accs, 1, 0, PART, CHUNK, "p1")
+
+        accs = {}
+        for side in range(2):
+            for t in range(PACK):
+                accs[side, t] = bank(PACK * side + t, [P, CHUNK])
+                for a in range(PASSES):
+                    first_pass(accs[side, t], side, a, t, 1)
+        empty(accs, 0, 1, 0, CHUNK, "q2")
+        empty(accs, 1, 1, 0, PART, "p2")
+        empty(accs, 1, 1, PART, CHUNK, "p3")
+
+        grouped0 = [work.tile([P, CHUNK, PACK], BF16, name=f"mixed0{w}", align_bytes=64) for w in range(2)]
+        for h in range(2):
+            mix(h, [g[:, h * PART : (h + 1) * PART, :] for g in grouped0])
+        operands0 = [quantise(f"chunk0{w}", grouped0[w][:], CHUNK) for w in range(2)]
+
+        def products0(n):
+            pair = (2 * n) % 8
+            y1, y2 = bank(pair, [P, CHUNK]), bank(pair + 1, [P, CHUNK])
+            second_pass(y1[:], 0, n, operands0[0])
+            second_pass(y2[:], 1, n, operands0[1])
+            return copy_out(f"0{n}", y1[:], [P, CHUNK]), y2
+
+        def finish0(n, made):
+            multiply(f"0{n}", made[0], made[1][:], [P, CHUNK], out[n * P : (n + 1) * P, 0:CHUNK])
+
+        grouped = {u: [work.tile([P, PART, PACK], BF16, name=f"mixed{u}{w}", align_bytes=64) for w in range(2)] for u in (2, 3)}
+        made0 = [products0(n) for n in range(4)]
+        mix(2, [g[:] for g in grouped[2]])
+        finish0(0, made0[0])
+        operands2 = [quantise(f"unit2{w}", grouped[2][w][:], PART) for w in range(2)]
+        made0.append(products0(4))
+        for n in range(1, N_TILES):
+            finish0(n, made0[n])
+
+        def products(unit, operands, banks):
+            first = [bank(banks[0], [P, 2, PART]), bank(banks[2], [P, 2, PART])]
+            second = [bank(banks[1], [P, 2, PART]), bank(banks[3], [P, 2, PART])]
+            last = bank(banks[4], [P, 2, PART])
+            made = []
+            for pair in range(2):
+                for i in range(2):
+                    second_pass(first[pair][:, i, :], 0, 2 * pair + i, operands[0])
+                for i in range(2):
+                    second_pass(second[pair][:, i, :], 1, 2 * pair + i, operands[1])
+                made.append((copy_out(f"{unit}{pair}", first[pair][:], [P, 2, PART]), second[pair][:]))
+            for which in range(2):
+                second_pass(last[:, which, :], which, 4, operands[which])
+            made.append((copy_out(f"{unit}2", last[:, 0, :], [P, PART]), last[:, 1, :]))
+            return made
+
+        def finish(unit, made):
+            cols = slice(unit * PART, (unit + 1) * PART)
+            for pair in range(2):
+                dest = out[2 * pair * P : 2 * (pair + 1) * P, cols].rearrange("(i p) j -> p i j", p=P)
+                multiply(f"{unit}{pair}", made[pair][0], made[pair][1], [P, 2, PART], dest)
+            multiply(f"{unit}2", made[2][0], made[2][1], [P, PART], out[4 * P : 5 * P, cols])
+
+        made2 = products(2, operands2, (2, 3, 4, 5, 6))
+        mix(3, [g[:] for g in grouped[3]])
+        operands3 = [quantise(f"unit3{w}", grouped[3][w][:], PART) for w in range(2)]
+        made3 = products(3, operands3, (0, 7, 2, 1, 4))
+        finish(2, made2)
+        finish(3, made3)

@@ -29,6 +29,7 @@ QUADS = 4
 SHIFT = 16
 HALF = H // 2
 PART = CHUNK // 2
+WD_PIECES = ((0, 384), (384, N))
 
 
 def tile_list_metaphor_spotting_kernel(
@@ -54,12 +55,12 @@ def tile_list_metaphor_spotting_kernel(
 
         lists = [keep.tile([P, S // 16], U16, name=f"list{side}") for side in range(2)]
         table_words = [keep.tile([P, T], U16, name=f"table_words{a}", align_bytes=64) for a in range(PASSES)]
-        nc.sync.dma_start(lists[0][:], offs2)
+        nc.sync.dma_start(lists[1][:], offs)
         nc.sync.dma_start(out=table_words[0][:].bitcast(I32), in_=tab_words[0].bitcast(I32))
         scale_rows = tab_scales.rearrange("a (q r) t -> r q a t", r=4)
         for r in range(4):
             nc.sync.dma_start(out=table_scales[r:P:SHIFT, :].bitcast(I32), in_=scale_rows[r].bitcast(I32))
-        nc.sync.dma_start(lists[1][:], offs)
+        nc.sync.dma_start(lists[0][:], offs2)
         wo_raw = keep.tile([P, PASSES, H], I32, name="wo_raw", align_bytes=64)
         nc.sync.dma_start(out=wo_raw[:], in_=wo_words.rearrange("a p c i -> p a (c i)").bitcast(I32))
         wo_rows = wo_scales.rearrange("a (q r) c -> r q a c", r=4)
@@ -85,18 +86,17 @@ def tile_list_metaphor_spotting_kernel(
             for c in range(CHUNKS):
                 picked[side, 0, c] = tile[:, c * CHUNK : (c + 1) * CHUNK]
 
-        gather_first(0)
-        for side in range(2):
-            nc.vector.tensor_copy(picked_scales[:, side * S : (side + 1) * S], table_scales[:].indirect(lists[side][:]))
         gather_first(1)
+        for side in (1, 0):
+            nc.vector.tensor_copy(picked_scales[:, side * S : (side + 1) * S], table_scales[:].indirect(lists[side][:]))
+        gather_first(0)
         nc.sync.dma_start(out=moved[0 : P - SHIFT, :].bitcast(I32), in_=picked_scales[SHIFT:P, :].bitcast(I32))
         table_planes = (picked_scales, moved)
 
         wd_raw = []
-        for h in range(2):
-            tile = work.tile([P, PACK, N // 2], F32, name=f"wd_raw{h}", tag=f"wd_raw{h}")
-            cols = wd[:, h * (N // 2) : (h + 1) * (N // 2)]
-            nc.sync.dma_start(out=tile[:], in_=cols.rearrange("(p j) n -> p j n", j=PACK))
+        for lo, hi in WD_PIECES:
+            tile = keep.tile([P, PACK, hi - lo], F32, name=f"wd_raw{lo}")
+            nc.sync.dma_start(out=tile[:], in_=wd[:, lo:hi].rearrange("(p j) n -> p j n", j=PACK))
             wd_raw.append(tile)
         biases = []
         for side, src in enumerate((bo, bv)):
@@ -109,16 +109,20 @@ def tile_list_metaphor_spotting_kernel(
         for r in range(4):
             nc.sync.dma_start(out=ws_plane[r:P:32, :].bitcast(I32), in_=ws_rows[r].bitcast(I32))
 
-        wo_codes = keep.tile([P, PASSES, H], I32, name="wo_codes", align_bytes=64)
-        nc.vector.tensor_copy(
-            out=wo_codes[:].rearrange("p a (t g i) -> p a g t i", t=PACK, i=4),
-            in_=wo_raw[:].rearrange("p a (g i t) -> p a g t i", t=PACK, i=4),
-        )
-        wo_plane = keep.tile([P, PASSES, H], U8, name="wo_plane", align_bytes=64)
-        nc.vector.tensor_copy(
-            out=wo_plane[:].rearrange("p a (t g i) -> p a g t i", t=PACK, i=16),
-            in_=wo_scales_raw[:].rearrange("p (a g i t) -> p a g t i", a=PASSES, t=PACK, i=16),
-        )
+        wo_codes, wo_plane = [], []
+        for a in range(PASSES):
+            codes = keep.tile([P, H], I32, name=f"wo_codes{a}", align_bytes=64)
+            nc.gpsimd.tensor_copy(
+                out=codes[:].rearrange("p (t m) -> p t m", t=PACK),
+                in_=wo_raw[:, a, :].rearrange("p (m t) -> p t m", t=PACK),
+            )
+            plane = keep.tile([P, H], U8, name=f"wo_plane{a}", align_bytes=64)
+            nc.gpsimd.tensor_copy(
+                out=plane[:].rearrange("p (t m) -> p t m", t=PACK),
+                in_=wo_scales_raw[:, a * H : (a + 1) * H].rearrange("p (m t) -> p t m", t=PACK),
+            )
+            wo_codes.append(codes)
+            wo_plane.append(plane)
 
         wv_codes, wv_plane = [], []
         for a in range(PASSES):
@@ -144,11 +148,14 @@ def tile_list_metaphor_spotting_kernel(
                 picked[side, 1, c] = part
 
         wd_grouped = keep.tile([P, N, PACK], BF16, name="wd_grouped", align_bytes=64)
-        for h in range(2):
-            part = wd_grouped[:, h * (N // 2) : (h + 1) * (N // 2), :]
-            nc.scalar.copy(
-                out=part.rearrange("p (g i) j -> p g j i", i=4),
-                in_=wd_raw[h][:].rearrange("p j (g i) -> p g j i", i=4),
+        for (lo, hi), raw in zip(WD_PIECES, wd_raw):
+            nc.gpsimd.tensor_scalar(
+                out=wd_grouped[:, lo:hi, :],
+                in0=raw[:].rearrange("p j n -> p n j"),
+                scalar1=1.0,
+                scalar2=0.0,
+                op0=MULT,
+                op1=ADD,
             )
         wd_codes = keep.tile([P, N], U32, name="wd_codes", align_bytes=64)
         wd_plane = keep.tile([P, N], U8, name="wd_plane", align_bytes=64)
@@ -162,7 +169,7 @@ def tile_list_metaphor_spotting_kernel(
         def weights(side, a, t):
             cols = slice(t * P, (t + 1) * P)
             if side == 0:
-                return wo_codes[:, a, cols], wo_plane[:, a, cols]
+                return wo_codes[a][:, cols], wo_plane[a][:, cols]
             return wv_codes[a][:, cols], wv_plane[a][:, cols]
 
         def first_pass(acc, side, a, t, c):
@@ -189,11 +196,11 @@ def tile_list_metaphor_spotting_kernel(
                 projected[side, 2 * c + h] = tile[:, :, h * PART - lo : (h + 1) * PART - lo]
 
         def mix(unit, grouped):
-            q_in = projected[0, unit].rearrange("p t (g i) -> p g t i", i=4)
-            p_in = projected[1, unit].rearrange("p t (g i) -> p g t i", i=4)
+            q_in = projected[0, unit].rearrange("p t (g i) -> p g t i", i=2)
+            p_in = projected[1, unit].rearrange("p t (g i) -> p g t i", i=2)
             for which, op in enumerate((ADD, SUBTRACT)):
                 nc.vector.tensor_tensor(
-                    out=grouped[which].rearrange("p (g i) t -> p g t i", i=4), in0=p_in, in1=q_in, op=op
+                    out=grouped[which].rearrange("p (g i) t -> p g t i", i=2), in0=p_in, in1=q_in, op=op
                 )
 
         def quantise(name, grouped, width):
@@ -230,7 +237,7 @@ def tile_list_metaphor_spotting_kernel(
                     if a == 0:
                         accs[side, t] = bank(PACK * side + t, [P, CHUNK])
                     first_pass(accs[side, t], side, a, t, 0)
-        empty(accs, 0, 0, 0, PART, "wd_raw1")
+        empty(accs, 0, 0, 0, PART, "q0")
         empty(accs, 1, 0, 0, PART, "p0")
         empty(accs, 0, 0, PART, CHUNK, "q1")
         empty(accs, 1, 0, PART, CHUNK, "p1")

@@ -29,7 +29,8 @@ QUADS = 4
 SHIFT = 16
 HALF = H // 2
 PART = CHUNK // 2
-WD_PIECES = ((0, 384), (384, N))
+WD_SPLIT = 384
+WD_PIECES = ((0, WD_SPLIT), (WD_SPLIT, N))
 
 
 def tile_list_metaphor_spotting_kernel(
@@ -55,12 +56,12 @@ def tile_list_metaphor_spotting_kernel(
 
         lists = [keep.tile([P, S // 16], U16, name=f"list{side}") for side in range(2)]
         table_words = [keep.tile([P, T], U16, name=f"table_words{a}", align_bytes=64) for a in range(PASSES)]
-        nc.sync.dma_start(lists[1][:], offs)
+        nc.sync.dma_start(lists[0][:], offs2)
         nc.sync.dma_start(out=table_words[0][:].bitcast(I32), in_=tab_words[0].bitcast(I32))
         scale_rows = tab_scales.rearrange("a (q r) t -> r q a t", r=4)
         for r in range(4):
             nc.sync.dma_start(out=table_scales[r:P:SHIFT, :].bitcast(I32), in_=scale_rows[r].bitcast(I32))
-        nc.sync.dma_start(lists[0][:], offs2)
+        nc.sync.dma_start(lists[1][:], offs)
         wo_raw = keep.tile([P, PASSES, H], I32, name="wo_raw", align_bytes=64)
         nc.sync.dma_start(out=wo_raw[:], in_=wo_words.rearrange("a p c i -> p a (c i)").bitcast(I32))
         wo_rows = wo_scales.rearrange("a (q r) c -> r q a c", r=4)
@@ -69,13 +70,19 @@ def tile_list_metaphor_spotting_kernel(
                 out=wo_scales_raw[r:P:32, :].bitcast(I32).rearrange("q (a c) -> q a c", a=PASSES),
                 in_=wo_rows[r].bitcast(I32),
             )
-        wv_raw = []
-        for a in range(PASSES):
-            tile = keep.tile([P, PACK, H], F32, name=f"wv_raw{a}")
-            rows = wv[a * K_PASS : (a + 1) * K_PASS, :]
-            nc.sync.dma_start(out=tile[:], in_=rows.rearrange("(p j) c -> p j c", j=PACK))
-            wv_raw.append(tile)
         nc.sync.dma_start(out=table_words[1][:].bitcast(I32), in_=tab_words[1].bitcast(I32))
+        biases = []
+        for side, src in enumerate((bo, bv)):
+            tile = keep.tile([P, PACK], F32, name=f"bias{side}")
+            nc.sync.dma_start(out=tile[:], in_=src.rearrange("(p t) -> p t", t=PACK))
+            biases.append(tile)
+        wv_raw = {}
+        for a in range(PASSES):
+            for h in range(2):
+                tile = work.tile([P, PACK, HALF], F32, name=f"wv_raw{a}{h}", tag=f"wv_raw{a}{h}", align_bytes=64)
+                rows = wv[a * K_PASS : (a + 1) * K_PASS, h * HALF : (h + 1) * HALF]
+                nc.sync.dma_start(out=tile[:], in_=rows.rearrange("(p j) c -> p j c", j=PACK))
+                wv_raw[a, h] = tile
 
         picked = {}
         picked_scales = keep.tile([P, 2 * S], U8, name="picked_scales", align_bytes=64)
@@ -86,10 +93,10 @@ def tile_list_metaphor_spotting_kernel(
             for c in range(CHUNKS):
                 picked[side, 0, c] = tile[:, c * CHUNK : (c + 1) * CHUNK]
 
-        gather_first(1)
-        for side in (1, 0):
-            nc.vector.tensor_copy(picked_scales[:, side * S : (side + 1) * S], table_scales[:].indirect(lists[side][:]))
         gather_first(0)
+        for side in range(2):
+            nc.vector.tensor_copy(picked_scales[:, side * S : (side + 1) * S], table_scales[:].indirect(lists[side][:]))
+        gather_first(1)
         nc.sync.dma_start(out=moved[0 : P - SHIFT, :].bitcast(I32), in_=picked_scales[SHIFT:P, :].bitcast(I32))
         table_planes = (picked_scales, moved)
 
@@ -98,11 +105,6 @@ def tile_list_metaphor_spotting_kernel(
             tile = keep.tile([P, PACK, hi - lo], F32, name=f"wd_raw{lo}")
             nc.sync.dma_start(out=tile[:], in_=wd[:, lo:hi].rearrange("(p j) n -> p j n", j=PACK))
             wd_raw.append(tile)
-        biases = []
-        for side, src in enumerate((bo, bv)):
-            tile = keep.tile([P, PACK], F32, name=f"bias{side}")
-            nc.sync.dma_start(out=tile[:], in_=src.rearrange("(p t) -> p t", t=PACK))
-            biases.append(tile)
         ws_codes = keep.tile([P, 2 * N], U8, name="ws_codes", align_bytes=64)
         nc.sync.dma_start(out=ws_codes[:].bitcast(I32), in_=ws_words[0].bitcast(I32))
         ws_rows = ws_scales[0].rearrange("(q r) n -> r q n", r=4)
@@ -127,10 +129,11 @@ def tile_list_metaphor_spotting_kernel(
         wv_codes, wv_plane = [], []
         for a in range(PASSES):
             grouped = work.tile([P, PACK, P, PACK], BF16, name=f"wv_grouped{a}", tag=f"wv_grouped{a}", align_bytes=64)
-            nc.scalar.copy(
-                out=grouped[:].rearrange("p t m j -> p m j t"),
-                in_=wv_raw[a][:].rearrange("p j (m t) -> p m j t", t=PACK),
-            )
+            for h in range(2):
+                nc.scalar.copy(
+                    out=grouped[:, :, h * (P // 2) : (h + 1) * (P // 2), :].rearrange("p t m j -> p m j t"),
+                    in_=wv_raw[a, h][:].rearrange("p j (m t) -> p m j t", t=PACK),
+                )
             codes = keep.tile([P, H], U32, name=f"wv_codes{a}", align_bytes=64)
             plane = keep.tile([P, H], U8, name=f"wv_plane{a}", align_bytes=64)
             nc.vector.quantize_mx(
@@ -139,32 +142,23 @@ def tile_list_metaphor_spotting_kernel(
             wv_codes.append(codes)
             wv_plane.append(plane)
 
-        second = work.tile([P, 2 * S], U16, name="picked_second", tag="wv_grouped1", align_bytes=64)
         for c in range(CHUNKS):
+            second = work.tile([P, 2 * CHUNK], U16, name=f"picked_second{c}", tag=f"wv_grouped{c}", align_bytes=64)
             for side in range(2):
-                part = second[:, (2 * c + side) * CHUNK : (2 * c + side + 1) * CHUNK]
+                part = second[:, side * CHUNK : (side + 1) * CHUNK]
                 cols = CHUNK // 16
                 nc.vector.tensor_copy(part, table_words[1][:].indirect(lists[side][:, c * cols : (c + 1) * cols]))
                 picked[side, 1, c] = part
 
-        wd_grouped = keep.tile([P, N, PACK], BF16, name="wd_grouped", align_bytes=64)
-        for (lo, hi), raw in zip(WD_PIECES, wd_raw):
-            nc.gpsimd.tensor_scalar(
-                out=wd_grouped[:, lo:hi, :],
-                in0=raw[:].rearrange("p j n -> p n j"),
-                scalar1=1.0,
-                scalar2=0.0,
-                op0=MULT,
-                op1=ADD,
-            )
-        wd_codes = keep.tile([P, N], U32, name="wd_codes", align_bytes=64)
-        wd_plane = keep.tile([P, N], U8, name="wd_plane", align_bytes=64)
-        for lo, hi in ((0, 512), (512, N)):
-            nc.vector.quantize_mx(
-                out=wd_codes[:, lo:hi].bitcast(FP8X4),
-                scales=wd_plane[:, lo:hi],
-                in_=wd_grouped[:, lo:hi, :].rearrange("p n j -> p (n j)"),
-            )
+        wd_first = keep.tile([P, WD_SPLIT, PACK], BF16, name="wd_first", align_bytes=64)
+        nc.gpsimd.tensor_scalar(
+            out=wd_first[:],
+            in0=wd_raw[0][:].rearrange("p j n -> p n j"),
+            scalar1=1.0,
+            scalar2=0.0,
+            op0=MULT,
+            op1=ADD,
+        )
 
         def weights(side, a, t):
             cols = slice(t * P, (t + 1) * P)
@@ -187,7 +181,7 @@ def tile_list_metaphor_spotting_kernel(
         projected = {}
 
         def empty(accs, side, c, lo, hi, tag):
-            tile = work.tile([P, PACK, hi - lo], F32, name=f"projected{side}{c}{lo}", tag=tag)
+            tile = work.tile([P, PACK, hi - lo], F32, name=f"projected{side}{c}{lo}", tag=tag, align_bytes=64)
             for t in range(PACK):
                 nc.scalar.activation(
                     out=tile[:, t, :], in_=accs[side, t][:, lo:hi], func=IDENTITY, bias=biases[side][:, t : t + 1]
@@ -237,10 +231,19 @@ def tile_list_metaphor_spotting_kernel(
                     if a == 0:
                         accs[side, t] = bank(PACK * side + t, [P, CHUNK])
                     first_pass(accs[side, t], side, a, t, 0)
-        empty(accs, 0, 0, 0, PART, "q0")
+        empty(accs, 0, 0, 0, PART, "wv_raw11")
         empty(accs, 1, 0, 0, PART, "p0")
         empty(accs, 0, 0, PART, CHUNK, "q1")
         empty(accs, 1, 0, PART, CHUNK, "p1")
+
+        grouped0 = [work.tile([P, CHUNK, PACK], BF16, name=f"mixed0{w}", align_bytes=64) for w in range(2)]
+        for h in range(2):
+            mix(h, [g[:, h * PART : (h + 1) * PART, :] for g in grouped0])
+        wd_rest = work.tile([P, N - WD_SPLIT, PACK], BF16, name="wd_rest", tag="wv_raw11", align_bytes=64)
+        nc.scalar.copy(
+            out=wd_rest[:].rearrange("p (g i) j -> p g j i", i=4),
+            in_=wd_raw[1][:].rearrange("p j (g i) -> p g j i", i=4),
+        )
 
         accs = {}
         for side in range(2):
@@ -252,10 +255,15 @@ def tile_list_metaphor_spotting_kernel(
         empty(accs, 1, 1, 0, PART, "p2")
         empty(accs, 1, 1, PART, CHUNK, "p3")
 
-        grouped0 = [work.tile([P, CHUNK, PACK], BF16, name=f"mixed0{w}", align_bytes=64) for w in range(2)]
-        for h in range(2):
-            mix(h, [g[:, h * PART : (h + 1) * PART, :] for g in grouped0])
         operands0 = [quantise(f"chunk0{w}", grouped0[w][:], CHUNK) for w in range(2)]
+        wd_codes = work.tile([P, N], U32, name="wd_codes", tag="p1", align_bytes=64)
+        wd_plane = keep.tile([P, N], U8, name="wd_plane", align_bytes=64)
+        for lo, hi, source in ((0, 256, wd_first[:, 0:256, :]), (256, WD_SPLIT, wd_first[:, 256:WD_SPLIT, :]), (WD_SPLIT, N, wd_rest[:])):
+            nc.vector.quantize_mx(
+                out=wd_codes[:, lo:hi].bitcast(FP8X4),
+                scales=wd_plane[:, lo:hi],
+                in_=source.rearrange("p n j -> p (n j)"),
+            )
 
         def products0(n):
             pair = (2 * n) % 8

@@ -24,13 +24,17 @@ K_PASS = P * PACK
 PASSES = K // K_PASS
 CHUNK = 512
 CHUNKS = S // CHUNK
-N_TILES = N // P
-QUADS = 4
+UNIT = CHUNK // 2
+QUAD = 32
+ROWS = 4
 SHIFT = 16
-HALF = H // 2
-PART = CHUNK // 2
+PER_COLUMN = 16
+LAST_TILE = N // P - 1
+SUM, DIFFERENCE = 0, 1
+WV_PIECES = (((0, H),), ((0, H // 2), (H // 2, H)))
 WD_SPLIT = 384
 WD_PIECES = ((0, WD_SPLIT), (WD_SPLIT, N))
+WD_CUT = 256
 
 
 def tile_list_metaphor_spotting_kernel(
@@ -49,69 +53,71 @@ def tile_list_metaphor_spotting_kernel(
         nc.vector.memset(table_scales[:].bitcast(I32), 0)
         wo_scales_raw = keep.tile([P, PASSES * H], U8, name="wo_scales_raw", align_bytes=64)
         nc.vector.memset(wo_scales_raw[:].bitcast(I32), 0)
-        moved = keep.tile([P, 2 * S], U8, name="moved", align_bytes=64)
-        nc.vector.memset(moved[:].bitcast(I32), 0)
+        shifted_scales = keep.tile([P, 2 * S], U8, name="shifted_scales", align_bytes=64)
+        nc.vector.memset(shifted_scales[:].bitcast(I32), 0)
         ws_plane = keep.tile([P, N], U8, name="ws_plane", align_bytes=64)
         nc.vector.memset(ws_plane[:].bitcast(I32), 0)
 
-        lists = [keep.tile([P, S // 16], U16, name=f"list{side}") for side in range(2)]
+        lists = [keep.tile([P, S // PER_COLUMN], U16, name=f"list{side}") for side in range(2)]
         table_words = [keep.tile([P, T], U16, name=f"table_words{a}", align_bytes=64) for a in range(PASSES)]
         nc.sync.dma_start(lists[0][:], offs2)
         nc.sync.dma_start(out=table_words[0][:].bitcast(I32), in_=tab_words[0].bitcast(I32))
-        scale_rows = tab_scales.rearrange("a (q r) t -> r q a t", r=4)
-        for r in range(4):
-            nc.sync.dma_start(out=table_scales[r:P:SHIFT, :].bitcast(I32), in_=scale_rows[r].bitcast(I32))
+        table_rows = tab_scales.rearrange("a (x y) t -> y x a t", y=ROWS)
+        for y in range(ROWS):
+            nc.sync.dma_start(out=table_scales[y:P:SHIFT, :].bitcast(I32), in_=table_rows[y].bitcast(I32))
         nc.sync.dma_start(lists[1][:], offs)
         wo_raw = keep.tile([P, PASSES, H], I32, name="wo_raw", align_bytes=64)
         nc.sync.dma_start(out=wo_raw[:], in_=wo_words.rearrange("a p c i -> p a (c i)").bitcast(I32))
-        wo_rows = wo_scales.rearrange("a (q r) c -> r q a c", r=4)
-        for r in range(4):
-            nc.sync.dma_start(
-                out=wo_scales_raw[r:P:32, :].bitcast(I32).rearrange("q (a c) -> q a c", a=PASSES),
-                in_=wo_rows[r].bitcast(I32),
+        wo_rows = wo_scales.rearrange("a (x y) c -> y x a c", y=ROWS)
+        for y in range(ROWS):
+            nc.gpsimd.dma_start(
+                out=wo_scales_raw[y:P:QUAD, :].bitcast(I32).rearrange("x (a c) -> x a c", a=PASSES),
+                in_=wo_rows[y].bitcast(I32),
             )
-        nc.sync.dma_start(out=table_words[1][:].bitcast(I32), in_=tab_words[1].bitcast(I32))
-        biases = []
-        for side, src in enumerate((bo, bv)):
-            tile = keep.tile([P, PACK], F32, name=f"bias{side}")
-            nc.sync.dma_start(out=tile[:], in_=src.rearrange("(p t) -> p t", t=PACK))
-            biases.append(tile)
         wv_raw = {}
-        for a in range(PASSES):
-            for h in range(2):
-                tile = work.tile([P, PACK, HALF], F32, name=f"wv_raw{a}{h}", tag=f"wv_raw{a}{h}", align_bytes=64)
-                rows = wv[a * K_PASS : (a + 1) * K_PASS, h * HALF : (h + 1) * HALF]
-                nc.sync.dma_start(out=tile[:], in_=rows.rearrange("(p j) c -> p j c", j=PACK))
-                wv_raw[a, h] = tile
+        for a, pieces in enumerate(WV_PIECES):
+            for lo, hi in pieces:
+                tile = work.tile([P, PACK, hi - lo], F32, name=f"wv_raw{a}{lo}", tag=f"wv_raw{a}{lo}", align_bytes=64)
+                rows = wv[a * K_PASS : (a + 1) * K_PASS, lo:hi]
+                nc.sync.dma_start(out=tile[:], in_=rows.rearrange("(p i) c -> p i c", i=PACK))
+                wv_raw[a, lo] = tile
+            if a == 0:
+                nc.sync.dma_start(out=table_words[1][:].bitcast(I32), in_=tab_words[1].bitcast(I32))
+        last_wv_tag = f"wv_raw1{H // 2}"
+        biases = []
+        for side, bias in enumerate((bo, bv)):
+            tile = keep.tile([P, PACK], F32, name=f"bias{side}")
+            nc.sync.dma_start(out=tile[:], in_=bias.rearrange("(m t) -> m t", t=PACK))
+            biases.append(tile)
 
         picked = {}
         picked_scales = keep.tile([P, 2 * S], U8, name="picked_scales", align_bytes=64)
 
-        def gather_first(side):
+        def gather_first_pass(side):
             tile = keep.tile([P, S], U16, name=f"picked{side}0", align_bytes=64)
             nc.vector.tensor_copy(tile[:], table_words[0][:].indirect(lists[side][:]))
             for c in range(CHUNKS):
                 picked[side, 0, c] = tile[:, c * CHUNK : (c + 1) * CHUNK]
 
-        gather_first(0)
+        gather_first_pass(0)
         for side in range(2):
             nc.vector.tensor_copy(picked_scales[:, side * S : (side + 1) * S], table_scales[:].indirect(lists[side][:]))
-        gather_first(1)
-        nc.sync.dma_start(out=moved[0 : P - SHIFT, :].bitcast(I32), in_=picked_scales[SHIFT:P, :].bitcast(I32))
-        table_planes = (picked_scales, moved)
+        gather_first_pass(1)
+        nc.sync.dma_start(out=shifted_scales[0 : P - SHIFT, :].bitcast(I32), in_=picked_scales[SHIFT:P, :].bitcast(I32))
+        table_planes = (picked_scales, shifted_scales)
 
         wd_raw = []
         for lo, hi in WD_PIECES:
             tile = keep.tile([P, PACK, hi - lo], F32, name=f"wd_raw{lo}")
-            nc.sync.dma_start(out=tile[:], in_=wd[:, lo:hi].rearrange("(p j) n -> p j n", j=PACK))
+            nc.sync.dma_start(out=tile[:], in_=wd[:, lo:hi].rearrange("(p i) n -> p i n", i=PACK))
             wd_raw.append(tile)
         ws_codes = keep.tile([P, 2 * N], U8, name="ws_codes", align_bytes=64)
         nc.sync.dma_start(out=ws_codes[:].bitcast(I32), in_=ws_words[0].bitcast(I32))
-        ws_rows = ws_scales[0].rearrange("(q r) n -> r q n", r=4)
-        for r in range(4):
-            nc.sync.dma_start(out=ws_plane[r:P:32, :].bitcast(I32), in_=ws_rows[r].bitcast(I32))
+        ws_rows = ws_scales[0].rearrange("(x y) n -> y x n", y=ROWS)
+        for y in range(ROWS):
+            nc.sync.dma_start(out=ws_plane[y:P:QUAD, :].bitcast(I32), in_=ws_rows[y].bitcast(I32))
 
-        wo_codes, wo_plane = [], []
+        wo_codes, wo_planes = [], []
         for a in range(PASSES):
             codes = keep.tile([P, H], I32, name=f"wo_codes{a}", align_bytes=64)
             nc.gpsimd.tensor_copy(
@@ -124,54 +130,52 @@ def tile_list_metaphor_spotting_kernel(
                 in_=wo_scales_raw[:, a * H : (a + 1) * H].rearrange("p (m t) -> p t m", t=PACK),
             )
             wo_codes.append(codes)
-            wo_plane.append(plane)
+            wo_planes.append(plane)
 
-        wv_codes, wv_plane = [], []
+        wv_codes, wv_planes = [], []
         for a in range(PASSES):
-            grouped = work.tile([P, PACK, P, PACK], BF16, name=f"wv_grouped{a}", tag=f"wv_grouped{a}", align_bytes=64)
-            for h in range(2):
+            wv_rounded = work.tile([P, PACK, P, PACK], BF16, name=f"wv_rounded{a}", tag=f"wv_rounded{a}", align_bytes=64)
+            for lo, hi in WV_PIECES[a]:
                 nc.scalar.copy(
-                    out=grouped[:, :, h * (P // 2) : (h + 1) * (P // 2), :].rearrange("p t m j -> p m j t"),
-                    in_=wv_raw[a, h][:].rearrange("p j (m t) -> p m j t", t=PACK),
+                    out=wv_rounded[:, :, lo // PACK : hi // PACK, :].rearrange("p t m i -> p m i t"),
+                    in_=wv_raw[a, lo][:].rearrange("p i (m t) -> p m i t", t=PACK),
                 )
             codes = keep.tile([P, H], U32, name=f"wv_codes{a}", align_bytes=64)
             plane = keep.tile([P, H], U8, name=f"wv_plane{a}", align_bytes=64)
             nc.vector.quantize_mx(
-                out=codes[:].bitcast(FP8X4), scales=plane[:], in_=grouped[:].rearrange("p t m j -> p (t m j)")
+                out=codes[:].bitcast(FP8X4), scales=plane[:], in_=wv_rounded[:].rearrange("p t m i -> p (t m i)")
             )
             wv_codes.append(codes)
-            wv_plane.append(plane)
+            wv_planes.append(plane)
 
+        columns = CHUNK // PER_COLUMN
         for c in range(CHUNKS):
-            second = work.tile([P, 2 * CHUNK], U16, name=f"picked_second{c}", tag=f"wv_grouped{c}", align_bytes=64)
+            tile = work.tile([P, 2 * CHUNK], U16, name=f"picked_second{c}", tag=f"wv_rounded{c}", align_bytes=64)
             for side in range(2):
-                part = second[:, side * CHUNK : (side + 1) * CHUNK]
-                cols = CHUNK // 16
-                nc.vector.tensor_copy(part, table_words[1][:].indirect(lists[side][:, c * cols : (c + 1) * cols]))
+                part = tile[:, side * CHUNK : (side + 1) * CHUNK]
+                offsets = lists[side][:, c * columns : (c + 1) * columns]
+                nc.vector.tensor_copy(part, table_words[1][:].indirect(offsets))
                 picked[side, 1, c] = part
 
         wd_first = keep.tile([P, WD_SPLIT, PACK], BF16, name="wd_first", align_bytes=64)
         nc.gpsimd.tensor_scalar(
             out=wd_first[:],
-            in0=wd_raw[0][:].rearrange("p j n -> p n j"),
+            in0=wd_raw[0][:].rearrange("p i n -> p n i"),
             scalar1=1.0,
             scalar2=0.0,
             op0=MULT,
             op1=ADD,
         )
 
-        def weights(side, a, t):
-            cols = slice(t * P, (t + 1) * P)
-            if side == 0:
-                return wo_codes[a][:, cols], wo_plane[a][:, cols]
-            return wv_codes[a][:, cols], wv_plane[a][:, cols]
+        first_weights = ((wo_codes, wo_planes), (wv_codes, wv_planes))
 
-        def first_pass(acc, side, a, t, c):
-            codes, plane = weights(side, a, t)
+        def project(acc, side, a, t, c):
+            codes, planes = first_weights[side]
+            cols = slice(t * P, (t + 1) * P)
             nc.tensor.matmul_mx(
                 out=acc[:],
-                lhsT=codes.bitcast(FP8X4),
-                lhsT_scale=plane,
+                lhsT=codes[a][:, cols].bitcast(FP8X4),
+                lhsT_scale=planes[a][:, cols],
                 rhs=picked[side, a, c].bitcast(FP4X4),
                 rhs_scale=table_planes[a][:, side * S + c * CHUNK : side * S + (c + 1) * CHUNK],
                 start=(a == 0),
@@ -186,43 +190,22 @@ def tile_list_metaphor_spotting_kernel(
                 nc.scalar.activation(
                     out=tile[:, t, :], in_=accs[side, t][:, lo:hi], func=IDENTITY, bias=biases[side][:, t : t + 1]
                 )
-            for h in range(lo // PART, hi // PART):
-                projected[side, 2 * c + h] = tile[:, :, h * PART - lo : (h + 1) * PART - lo]
+            for half in range(lo // UNIT, hi // UNIT):
+                projected[side, 2 * c + half] = tile[:, :, half * UNIT - lo : (half + 1) * UNIT - lo]
 
-        def mix(unit, grouped):
-            q_in = projected[0, unit].rearrange("p t (g i) -> p g t i", i=2)
-            p_in = projected[1, unit].rearrange("p t (g i) -> p g t i", i=2)
-            for which, op in enumerate((ADD, SUBTRACT)):
-                nc.vector.tensor_tensor(
-                    out=grouped[which].rearrange("p (g i) t -> p g t i", i=2), in0=p_in, in1=q_in, op=op
-                )
-
-        def quantise(name, grouped, width):
-            codes = work.tile([P, width], U32, name=f"{name}_codes", align_bytes=64)
-            plane = work.tile([P, width], U8, name=f"{name}_plane", align_bytes=64)
-            nc.vector.quantize_mx(out=codes[:].bitcast(FP8X4), scales=plane[:], in_=grouped.rearrange("p j t -> p (j t)"))
-            return codes, plane
-
-        def second_pass(acc, which, n, operand):
-            rows = slice(n * P, (n + 1) * P)
-            if which == 0:
-                lhs, lhs_plane = ws_codes[:, 2 * n * P : 2 * (n + 1) * P].bitcast(FP4X4), ws_plane[:, rows]
-            else:
-                lhs, lhs_plane = wd_codes[:, rows].bitcast(FP8X4), wd_plane[:, rows]
-            nc.tensor.matmul_mx(
-                out=acc, lhsT=lhs, lhsT_scale=lhs_plane, rhs=operand[0][:].bitcast(FP8X4), rhs_scale=operand[1][:],
-                start=True, stop=True,
+        def combine(unit, which, dest):
+            nc.vector.tensor_tensor(
+                out=dest.rearrange("p (g j) t -> p g t j", j=2),
+                in0=projected[1, unit].rearrange("p t (g j) -> p g t j", j=2),
+                in1=projected[0, unit].rearrange("p t (g j) -> p g t j", j=2),
+                op=(ADD, SUBTRACT)[which],
             )
 
-        def copy_out(name, y1, shape):
-            tile = work.tile(shape, F32, name=f"y1_{name}")
-            nc.scalar.copy(out=tile[:], in_=y1)
-            return tile
-
-        def multiply(name, y1_sb, y2, shape, dest):
-            result = work.tile(shape, F32, name=f"result_{name}")
-            nc.vector.tensor_tensor(out=result[:], in0=y2, in1=y1_sb[:], op=MULT)
-            nc.sync.dma_start(out=dest, in_=result[:])
+        def quantise(name, values, tokens):
+            codes = work.tile([P, tokens], U32, name=f"{name}_codes", align_bytes=64)
+            plane = work.tile([P, tokens], U8, name=f"{name}_plane", align_bytes=64)
+            nc.vector.quantize_mx(out=codes[:].bitcast(FP8X4), scales=plane[:], in_=values.rearrange("p j t -> p (j t)"))
+            return codes, plane
 
         accs = {}
         for a in range(PASSES):
@@ -230,19 +213,20 @@ def tile_list_metaphor_spotting_kernel(
                 for t in range(PACK):
                     if a == 0:
                         accs[side, t] = bank(PACK * side + t, [P, CHUNK])
-                    first_pass(accs[side, t], side, a, t, 0)
-        empty(accs, 0, 0, 0, PART, "wv_raw11")
-        empty(accs, 1, 0, 0, PART, "p0")
-        empty(accs, 0, 0, PART, CHUNK, "q1")
-        empty(accs, 1, 0, PART, CHUNK, "p1")
+                    project(accs[side, t], side, a, t, 0)
+        empty(accs, 0, 0, 0, UNIT, last_wv_tag)
+        empty(accs, 1, 0, 0, UNIT, "p0")
+        empty(accs, 0, 0, UNIT, CHUNK, "q1")
+        empty(accs, 1, 0, UNIT, CHUNK, "p1")
 
-        grouped0 = [work.tile([P, CHUNK, PACK], BF16, name=f"mixed0{w}", align_bytes=64) for w in range(2)]
-        for h in range(2):
-            mix(h, [g[:, h * PART : (h + 1) * PART, :] for g in grouped0])
-        wd_rest = work.tile([P, N - WD_SPLIT, PACK], BF16, name="wd_rest", tag="wv_raw11", align_bytes=64)
+        rounded0 = [work.tile([P, CHUNK, PACK], BF16, name=f"rounded0{which}", align_bytes=64) for which in range(2)]
+        for unit in range(2):
+            for which in range(2):
+                combine(unit, which, rounded0[which][:, unit * UNIT : (unit + 1) * UNIT, :])
+        wd_rest = work.tile([P, N - WD_SPLIT, PACK], BF16, name="wd_rest", tag=last_wv_tag, align_bytes=64)
         nc.scalar.copy(
-            out=wd_rest[:].rearrange("p (g i) j -> p g j i", i=4),
-            in_=wd_raw[1][:].rearrange("p j (g i) -> p g j i", i=4),
+            out=wd_rest[:].rearrange("p (g n) i -> p g i n", n=4),
+            in_=wd_raw[1][:].rearrange("p i (g n) -> p g i n", n=4),
         )
 
         accs = {}
@@ -250,66 +234,125 @@ def tile_list_metaphor_spotting_kernel(
             for t in range(PACK):
                 accs[side, t] = bank(PACK * side + t, [P, CHUNK])
                 for a in range(PASSES):
-                    first_pass(accs[side, t], side, a, t, 1)
+                    project(accs[side, t], side, a, t, 1)
         empty(accs, 0, 1, 0, CHUNK, "q2")
-        empty(accs, 1, 1, 0, PART, "p2")
-        empty(accs, 1, 1, PART, CHUNK, "p3")
+        empty(accs, 1, 1, 0, UNIT, "p2")
+        empty(accs, 1, 1, UNIT, CHUNK, "p3")
 
-        operands0 = [quantise(f"chunk0{w}", grouped0[w][:], CHUNK) for w in range(2)]
+        operands0 = [quantise(f"chunk0{which}", rounded0[which][:], CHUNK) for which in range(2)]
         wd_codes = work.tile([P, N], U32, name="wd_codes", tag="p1", align_bytes=64)
         wd_plane = keep.tile([P, N], U8, name="wd_plane", align_bytes=64)
-        for lo, hi, source in ((0, 256, wd_first[:, 0:256, :]), (256, WD_SPLIT, wd_first[:, 256:WD_SPLIT, :]), (WD_SPLIT, N, wd_rest[:])):
+        wd_parts = (
+            (0, WD_CUT, wd_first[:, 0:WD_CUT, :]),
+            (WD_CUT, WD_SPLIT, wd_first[:, WD_CUT:WD_SPLIT, :]),
+            (WD_SPLIT, N, wd_rest[:]),
+        )
+        for lo, hi, values in wd_parts:
             nc.vector.quantize_mx(
                 out=wd_codes[:, lo:hi].bitcast(FP8X4),
                 scales=wd_plane[:, lo:hi],
-                in_=source.rearrange("p n j -> p (n j)"),
+                in_=values.rearrange("p n i -> p (n i)"),
             )
 
-        def products0(n):
-            pair = (2 * n) % 8
-            y1, y2 = bank(pair, [P, CHUNK]), bank(pair + 1, [P, CHUNK])
-            second_pass(y1[:], 0, n, operands0[0])
-            second_pass(y2[:], 1, n, operands0[1])
-            return copy_out(f"0{n}", y1[:], [P, CHUNK]), y2
+        def product(acc, which, n, operand):
+            rows = slice(n * P, (n + 1) * P)
+            if which == SUM:
+                codes, plane = ws_codes[:, 2 * n * P : 2 * (n + 1) * P].bitcast(FP4X4), ws_plane[:, rows]
+            else:
+                codes, plane = wd_codes[:, rows].bitcast(FP8X4), wd_plane[:, rows]
+            nc.tensor.matmul_mx(
+                out=acc,
+                lhsT=codes,
+                lhsT_scale=plane,
+                rhs=operand[0][:].bitcast(FP8X4),
+                rhs_scale=operand[1][:],
+                start=True,
+                stop=True,
+            )
 
-        def finish0(n, made):
-            multiply(f"0{n}", made[0], made[1][:], [P, CHUNK], out[n * P : (n + 1) * P, 0:CHUNK])
+        def copy_out(name, acc, shape):
+            tile = work.tile(shape, F32, name=f"copy_{name}")
+            nc.scalar.copy(out=tile[:], in_=acc)
+            return tile
 
-        grouped = {u: [work.tile([P, PART, PACK], BF16, name=f"mixed{u}{w}", align_bytes=64) for w in range(2)] for u in (2, 3)}
-        made0 = [products0(n) for n in range(4)]
-        mix(2, [g[:] for g in grouped[2]])
-        finish0(0, made0[0])
-        operands2 = [quantise(f"unit2{w}", grouped[2][w][:], PART) for w in range(2)]
-        made0.append(products0(4))
-        for n in range(1, N_TILES):
-            finish0(n, made0[n])
+        def multiply(name, y1_copy, y2, shape, dest):
+            result = work.tile(shape, F32, name=f"result_{name}")
+            nc.vector.tensor_tensor(out=result[:], in0=y2, in1=y1_copy[:], op=MULT)
+            nc.sync.dma_start(out=dest, in_=result[:])
 
-        def products(unit, operands, banks):
-            first = [bank(banks[0], [P, 2, PART]), bank(banks[2], [P, 2, PART])]
-            second = [bank(banks[1], [P, 2, PART]), bank(banks[3], [P, 2, PART])]
-            last = bank(banks[4], [P, 2, PART])
-            made = []
-            for pair in range(2):
-                for i in range(2):
-                    second_pass(first[pair][:, i, :], 0, 2 * pair + i, operands[0])
-                for i in range(2):
-                    second_pass(second[pair][:, i, :], 1, 2 * pair + i, operands[1])
-                made.append((copy_out(f"{unit}{pair}", first[pair][:], [P, 2, PART]), second[pair][:]))
-            for which in range(2):
-                second_pass(last[:, which, :], which, 4, operands[which])
-            made.append((copy_out(f"{unit}2", last[:, 0, :], [P, PART]), last[:, 1, :]))
-            return made
+        def tile_products(n):
+            index = 2 * n % 8
+            y1 = bank(index, [P, CHUNK])
+            product(y1[:], SUM, n, operands0[SUM])
+            y1_copy = copy_out(f"y1_0{n}", y1[:], [P, CHUNK])
+            y2 = bank(index + 1, [P, CHUNK])
+            product(y2[:], DIFFERENCE, n, operands0[DIFFERENCE])
+            return y1_copy, y2[:]
 
-        def finish(unit, made):
-            cols = slice(unit * PART, (unit + 1) * PART)
-            for pair in range(2):
-                dest = out[2 * pair * P : 2 * (pair + 1) * P, cols].rearrange("(i p) j -> p i j", p=P)
-                multiply(f"{unit}{pair}", made[pair][0], made[pair][1], [P, 2, PART], dest)
-            multiply(f"{unit}2", made[2][0], made[2][1], [P, PART], out[4 * P : 5 * P, cols])
+        def finish_tile(n, made):
+            multiply(f"0{n}", made[0], made[1], [P, CHUNK], out[n * P : (n + 1) * P, 0:CHUNK])
 
-        made2 = products(2, operands2, (2, 3, 4, 5, 6))
-        mix(3, [g[:] for g in grouped[3]])
-        operands3 = [quantise(f"unit3{w}", grouped[3][w][:], PART) for w in range(2)]
-        made3 = products(3, operands3, (0, 7, 2, 1, 4))
-        finish(2, made2)
-        finish(3, made3)
+        def pair_product(which, pair, index, operand):
+            acc = bank(index, [P, 2, UNIT])
+            for i in range(2):
+                product(acc[:, i, :], which, 2 * pair + i, operand)
+            return acc[:]
+
+        def finish_pair(unit, pair, y1_copy, y2):
+            dest = out[2 * pair * P : 2 * (pair + 1) * P, unit * UNIT : (unit + 1) * UNIT]
+            multiply(f"{unit}{pair}", y1_copy, y2, [P, 2, UNIT], dest.rearrange("(i p) j -> p i j", p=P))
+
+        def finish_last(unit, y1_copy, y2):
+            dest = out[LAST_TILE * P : N, unit * UNIT : (unit + 1) * UNIT]
+            multiply(f"{unit}last", y1_copy, y2, [P, UNIT], dest)
+
+        rounded1 = {
+            unit: [
+                work.tile([P, UNIT, PACK], BF16, name=f"rounded{unit}{w}", tag=f"rounded{unit}{w}", align_bytes=64)
+                for w in range(2)
+            ]
+            for unit in (2, 3)
+        }
+        y1_00, y2_00 = tile_products(0)
+        for which in range(2):
+            combine(2, which, rounded1[2][which][:])
+        operands2 = [quantise(f"unit2{which}", rounded1[2][which][:], UNIT) for which in range(2)]
+
+        y2_00_copy = copy_out("y2_00", y2_00, [P, CHUNK])
+        result_00 = work.tile([P, CHUNK], F32, name="result_00", tag="rounded21", align_bytes=64)
+        nc.gpsimd.tensor_tensor(out=result_00[:], in0=y2_00_copy[:], in1=y1_00[:], op=MULT)
+        nc.sync.dma_start(out=out[0:P, 0:CHUNK], in_=result_00[:])
+
+        tiles0 = {n: tile_products(n) for n in range(1, LAST_TILE + 1)}
+        for n in range(1, LAST_TILE):
+            finish_tile(n, tiles0[n])
+
+        combine(3, SUM, rounded1[3][SUM][:])
+        y1_20 = copy_out("y1_20", pair_product(SUM, 0, 2, operands2[SUM]), [P, 2, UNIT])
+        y2_20 = pair_product(DIFFERENCE, 0, 3, operands2[DIFFERENCE])
+        last2 = bank(6, [P, 2, UNIT])
+        for which in range(2):
+            product(last2[:, which, :], which, LAST_TILE, operands2[which])
+        y1_2last = copy_out("y1_2last", last2[:, SUM, :], [P, UNIT])
+        y1_21 = copy_out("y1_21", pair_product(SUM, 1, 4, operands2[SUM]), [P, 2, UNIT])
+        y2_21 = pair_product(DIFFERENCE, 1, 5, operands2[DIFFERENCE])
+
+        finish_tile(LAST_TILE, tiles0[LAST_TILE])
+        sums3 = quantise("unit30", rounded1[3][SUM][:], UNIT)
+        y1_30 = copy_out("y1_30", pair_product(SUM, 0, 0, sums3), [P, 2, UNIT])
+        y1_31 = copy_out("y1_31", pair_product(SUM, 1, 2, sums3), [P, 2, UNIT])
+        last3 = bank(4, [P, 2, UNIT])
+        product(last3[:, SUM, :], SUM, LAST_TILE, sums3)
+        y1_3last = copy_out("y1_3last", last3[:, SUM, :], [P, UNIT])
+        combine(3, DIFFERENCE, rounded1[3][DIFFERENCE][:])
+        finish_last(2, y1_2last, last2[:, DIFFERENCE, :])
+        differences3 = quantise("unit31", rounded1[3][DIFFERENCE][:], UNIT)
+        y2_30 = pair_product(DIFFERENCE, 0, 7, differences3)
+        y2_31 = pair_product(DIFFERENCE, 1, 1, differences3)
+        product(last3[:, DIFFERENCE, :], DIFFERENCE, LAST_TILE, differences3)
+
+        finish_pair(2, 0, y1_20, y2_20)
+        finish_pair(2, 1, y1_21, y2_21)
+        finish_pair(3, 0, y1_30, y2_30)
+        finish_pair(3, 1, y1_31, y2_31)
+        finish_last(3, y1_3last, last3[:, DIFFERENCE, :])

@@ -27,14 +27,13 @@ CHUNKS = S // CHUNK
 UNIT = CHUNK // 2
 QUAD = 32
 ROWS = 4
-SHIFT = 16
+SCALE_BASE = P - PASSES * 16
 PER_COLUMN = 16
 LAST_TILE = N // P - 1
 SUM, DIFFERENCE = 0, 1
-WV_PIECES = (((0, H),), ((0, H // 2), (H // 2, H)))
-WD_SPLIT = 384
-WD_PIECES = ((0, WD_SPLIT), (WD_SPLIT, N))
-WD_CUT = 256
+WD_SPLIT = 512
+WD_PIECES = ((0, 256), (256, WD_SPLIT), (WD_SPLIT, N))
+VERB, OBJECT = 1, 0
 
 
 def tile_list_metaphor_spotting_kernel(
@@ -49,62 +48,56 @@ def tile_list_metaphor_spotting_kernel(
         def bank(index, shape):
             return psum.tile(shape, F32, name=f"bank{index}", tag=f"bank{index}")
 
-        table_scales = keep.tile([P, T], U8, name="table_scales", align_bytes=64)
-        nc.vector.memset(table_scales[:].bitcast(I32), 0)
+        table_scales = work.tile([P, T], U8, name="table_scales", tag="table_late", align_bytes=64)
+        nc.vector.memset(table_scales[0:SCALE_BASE, :].bitcast(I32), 0)
+        table_planes = keep.tile([P, PASSES * 2 * S], U8, name="table_planes", align_bytes=64)
+        nc.vector.memset(table_planes[:].bitcast(I32), 0)
         wo_scales_raw = keep.tile([P, PASSES * H], U8, name="wo_scales_raw", align_bytes=64)
         nc.vector.memset(wo_scales_raw[:].bitcast(I32), 0)
-        shifted_scales = keep.tile([P, 2 * S], U8, name="shifted_scales", align_bytes=64)
-        nc.vector.memset(shifted_scales[:].bitcast(I32), 0)
         ws_plane = keep.tile([P, N], U8, name="ws_plane", align_bytes=64)
         nc.vector.memset(ws_plane[:].bitcast(I32), 0)
 
         lists = [keep.tile([P, S // PER_COLUMN], U16, name=f"list{side}") for side in range(2)]
-        table_words = [keep.tile([P, T], U16, name=f"table_words{a}", align_bytes=64) for a in range(PASSES)]
-        nc.sync.dma_start(lists[0][:], offs2)
+        nc.sync.dma_start(lists[VERB][:], offs)
+        nc.sync.dma_start(
+            out=table_scales[SCALE_BASE:P, :].bitcast(I32), in_=tab_scales.rearrange("a q t -> q a t").bitcast(I32)
+        )
+        nc.sync.dma_start(lists[OBJECT][:], offs2)
+        table_words = [keep.tile([P, T], U16, name="table_words0", align_bytes=64)]
         nc.sync.dma_start(out=table_words[0][:].bitcast(I32), in_=tab_words[0].bitcast(I32))
-        table_rows = tab_scales.rearrange("a (x y) t -> y x a t", y=ROWS)
-        for y in range(ROWS):
-            nc.sync.dma_start(out=table_scales[y:P:SHIFT, :].bitcast(I32), in_=table_rows[y].bitcast(I32))
-        nc.sync.dma_start(lists[1][:], offs)
-        wo_raw = keep.tile([P, PASSES, H], I32, name="wo_raw", align_bytes=64)
-        nc.sync.dma_start(out=wo_raw[:], in_=wo_words.rearrange("a p c i -> p a (c i)").bitcast(I32))
         wo_rows = wo_scales.rearrange("a (x y) c -> y x a c", y=ROWS)
         for y in range(ROWS):
             nc.gpsimd.dma_start(
                 out=wo_scales_raw[y:P:QUAD, :].bitcast(I32).rearrange("x (a c) -> x a c", a=PASSES),
                 in_=wo_rows[y].bitcast(I32),
             )
-        wv_raw = {}
-        for a, pieces in enumerate(WV_PIECES):
-            for lo, hi in pieces:
-                tile = work.tile([P, PACK, hi - lo], F32, name=f"wv_raw{a}{lo}", tag=f"wv_raw{a}{lo}", align_bytes=64)
-                rows = wv[a * K_PASS : (a + 1) * K_PASS, lo:hi]
-                nc.sync.dma_start(out=tile[:], in_=rows.rearrange("(p i) c -> p i c", i=PACK))
-                wv_raw[a, lo] = tile
-            if a == 0:
-                nc.sync.dma_start(out=table_words[1][:].bitcast(I32), in_=tab_words[1].bitcast(I32))
-        last_wv_tag = f"wv_raw1{H // 2}"
+        wv_raw = []
+        for a in range(PASSES):
+            tile = keep.tile([P, PACK, H], F32, name=f"wv_raw{a}", align_bytes=64)
+            rows = wv[a * K_PASS : (a + 1) * K_PASS, :]
+            nc.sync.dma_start(out=tile[:], in_=rows.rearrange("(p i) c -> p i c", i=PACK))
+            wv_raw.append(tile)
+        wo_raw = [keep.tile([P, H], I32, name="wo_raw0", align_bytes=64)]
+        nc.sync.dma_start(out=wo_raw[0][:], in_=wo_words[0].rearrange("p c i -> p (c i)").bitcast(I32))
+
+        picked_scales = work.tile([P, 2 * S], U8, name="picked_scales", tag="wo_late", align_bytes=64)
+        for side in (VERB, OBJECT):
+            nc.vector.tensor_copy(picked_scales[:, side * S : (side + 1) * S], table_scales[:].indirect(lists[side][:]))
+        for x in range(P // QUAD):
+            first = SCALE_BASE + PASSES * ROWS * x
+            nc.sync.dma_start(
+                out=table_planes[QUAD * x : QUAD * x + ROWS, :].bitcast(I32).rearrange("y (a c) -> y a c", a=PASSES),
+                in_=picked_scales[first : first + PASSES * ROWS, :].bitcast(I32),
+            )
+        table_words.append(work.tile([P, T], U16, name="table_words1", tag="table_late", align_bytes=64))
+        nc.sync.dma_start(out=table_words[1][:].bitcast(I32), in_=tab_words[1].bitcast(I32))
+        wo_raw.append(work.tile([P, H], I32, name="wo_raw1", tag="wo_late", align_bytes=64))
+        nc.sync.dma_start(out=wo_raw[1][:], in_=wo_words[1].rearrange("p c i -> p (c i)").bitcast(I32))
         biases = []
         for side, bias in enumerate((bo, bv)):
             tile = keep.tile([P, PACK], F32, name=f"bias{side}")
             nc.sync.dma_start(out=tile[:], in_=bias.rearrange("(m t) -> m t", t=PACK))
             biases.append(tile)
-
-        picked = {}
-        picked_scales = keep.tile([P, 2 * S], U8, name="picked_scales", align_bytes=64)
-
-        def gather_first_pass(side):
-            tile = keep.tile([P, S], U16, name=f"picked{side}0", align_bytes=64)
-            nc.vector.tensor_copy(tile[:], table_words[0][:].indirect(lists[side][:]))
-            for c in range(CHUNKS):
-                picked[side, 0, c] = tile[:, c * CHUNK : (c + 1) * CHUNK]
-
-        gather_first_pass(0)
-        for side in range(2):
-            nc.vector.tensor_copy(picked_scales[:, side * S : (side + 1) * S], table_scales[:].indirect(lists[side][:]))
-        gather_first_pass(1)
-        nc.sync.dma_start(out=shifted_scales[0 : P - SHIFT, :].bitcast(I32), in_=picked_scales[SHIFT:P, :].bitcast(I32))
-        table_planes = (picked_scales, shifted_scales)
 
         wd_raw = []
         for lo, hi in WD_PIECES:
@@ -117,29 +110,36 @@ def tile_list_metaphor_spotting_kernel(
         for y in range(ROWS):
             nc.sync.dma_start(out=ws_plane[y:P:QUAD, :].bitcast(I32), in_=ws_rows[y].bitcast(I32))
 
-        wo_codes, wo_planes = [], []
+        wo_planes = []
         for a in range(PASSES):
-            codes = keep.tile([P, H], I32, name=f"wo_codes{a}", align_bytes=64)
-            nc.gpsimd.tensor_copy(
-                out=codes[:].rearrange("p (t m) -> p t m", t=PACK),
-                in_=wo_raw[:, a, :].rearrange("p (m t) -> p t m", t=PACK),
-            )
             plane = keep.tile([P, H], U8, name=f"wo_plane{a}", align_bytes=64)
             nc.gpsimd.tensor_copy(
                 out=plane[:].rearrange("p (t m) -> p t m", t=PACK),
                 in_=wo_scales_raw[:, a * H : (a + 1) * H].rearrange("p (m t) -> p t m", t=PACK),
             )
-            wo_codes.append(codes)
             wo_planes.append(plane)
+
+        picked = {}
+        columns = CHUNK // PER_COLUMN
+
+        def gather_chunk(dest, side, a, c):
+            nc.vector.tensor_copy(dest, table_words[a][:].indirect(lists[side][:, c * columns : (c + 1) * columns]))
+            picked[side, a, c] = dest
+
+        verbs_first = keep.tile([P, S], U16, name="verbs_first", align_bytes=64)
+        nc.vector.tensor_copy(verbs_first[:], table_words[0][:].indirect(lists[VERB][:]))
+        for c in range(CHUNKS):
+            picked[VERB, 0, c] = verbs_first[:, c * CHUNK : (c + 1) * CHUNK]
+        objects_first = keep.tile([P, CHUNK], U16, name="objects_first", align_bytes=64)
+        gather_chunk(objects_first[:], OBJECT, 0, 0)
 
         wv_codes, wv_planes = [], []
         for a in range(PASSES):
             wv_rounded = work.tile([P, PACK, P, PACK], BF16, name=f"wv_rounded{a}", tag=f"wv_rounded{a}", align_bytes=64)
-            for lo, hi in WV_PIECES[a]:
-                nc.scalar.copy(
-                    out=wv_rounded[:, :, lo // PACK : hi // PACK, :].rearrange("p t m i -> p m i t"),
-                    in_=wv_raw[a, lo][:].rearrange("p i (m t) -> p m i t", t=PACK),
-                )
+            nc.scalar.copy(
+                out=wv_rounded[:].rearrange("p t m i -> p m i t"),
+                in_=wv_raw[a][:].rearrange("p i (m t) -> p m i t", t=PACK),
+            )
             codes = keep.tile([P, H], U32, name=f"wv_codes{a}", align_bytes=64)
             plane = keep.tile([P, H], U8, name=f"wv_plane{a}", align_bytes=64)
             nc.vector.quantize_mx(
@@ -147,25 +147,36 @@ def tile_list_metaphor_spotting_kernel(
             )
             wv_codes.append(codes)
             wv_planes.append(plane)
+            if a == 0:
+                objects_rest = work.tile([P, CHUNK], U16, name="objects_rest", tag="wv_rounded0", align_bytes=64)
+                gather_chunk(objects_rest[:], OBJECT, 0, 1)
 
-        columns = CHUNK // PER_COLUMN
+        wo_codes = []
+        for a in range(PASSES):
+            codes = keep.tile([P, H], U32, name=f"wo_codes{a}", align_bytes=64)
+            nc.scalar.copy(
+                out=codes[:].rearrange("p (t m) -> p m t", t=PACK),
+                in_=wo_raw[a][:].bitcast(U32).rearrange("p (m t) -> p m t", t=PACK),
+            )
+            wo_codes.append(codes)
+
+        picked_second = work.tile([P, 2 * S], U16, name="picked_second", tag="wv_rounded1", align_bytes=64)
         for c in range(CHUNKS):
-            tile = work.tile([P, 2 * CHUNK], U16, name=f"picked_second{c}", tag=f"wv_rounded{c}", align_bytes=64)
-            for side in range(2):
-                part = tile[:, side * CHUNK : (side + 1) * CHUNK]
-                offsets = lists[side][:, c * columns : (c + 1) * columns]
-                nc.vector.tensor_copy(part, table_words[1][:].indirect(offsets))
-                picked[side, 1, c] = part
+            for place, side in enumerate((VERB, OBJECT)):
+                lo = (2 * c + place) * CHUNK
+                gather_chunk(picked_second[:, lo : lo + CHUNK], side, 1, c)
 
         wd_first = keep.tile([P, WD_SPLIT, PACK], BF16, name="wd_first", align_bytes=64)
-        nc.gpsimd.tensor_scalar(
-            out=wd_first[:],
-            in0=wd_raw[0][:].rearrange("p i n -> p n i"),
-            scalar1=1.0,
-            scalar2=0.0,
-            op0=MULT,
-            op1=ADD,
-        )
+        for piece in range(2):
+            lo, hi = WD_PIECES[piece]
+            nc.gpsimd.tensor_scalar(
+                out=wd_first[:, lo:hi, :],
+                in0=wd_raw[piece][:].rearrange("p i n -> p n i"),
+                scalar1=1.0,
+                scalar2=0.0,
+                op0=MULT,
+                op1=ADD,
+            )
 
         first_weights = ((wo_codes, wo_planes), (wv_codes, wv_planes))
 
@@ -177,7 +188,7 @@ def tile_list_metaphor_spotting_kernel(
                 lhsT=codes[a][:, cols].bitcast(FP8X4),
                 lhsT_scale=planes[a][:, cols],
                 rhs=picked[side, a, c].bitcast(FP4X4),
-                rhs_scale=table_planes[a][:, side * S + c * CHUNK : side * S + (c + 1) * CHUNK],
+                rhs_scale=table_planes[:, (2 * a + side) * S + c * CHUNK : (2 * a + side) * S + (c + 1) * CHUNK],
                 start=(a == 0),
                 stop=(a == PASSES - 1),
             )
@@ -209,42 +220,41 @@ def tile_list_metaphor_spotting_kernel(
 
         accs = {}
         for a in range(PASSES):
-            for side in range(2):
+            for side in (VERB, OBJECT):
                 for t in range(PACK):
                     if a == 0:
-                        accs[side, t] = bank(PACK * side + t, [P, CHUNK])
+                        accs[side, t] = bank(PACK * (1 - side) + t, [P, CHUNK])
                     project(accs[side, t], side, a, t, 0)
-        empty(accs, 0, 0, 0, UNIT, last_wv_tag)
-        empty(accs, 1, 0, 0, UNIT, "p0")
-        empty(accs, 0, 0, UNIT, CHUNK, "q1")
-        empty(accs, 1, 0, UNIT, CHUNK, "p1")
+        empty(accs, VERB, 0, 0, UNIT, "p0")
+        empty(accs, OBJECT, 0, 0, UNIT, "q0")
+        empty(accs, VERB, 0, UNIT, CHUNK, "p1")
+        empty(accs, OBJECT, 0, UNIT, CHUNK, "q1")
 
         rounded0 = [work.tile([P, CHUNK, PACK], BF16, name=f"rounded0{which}", align_bytes=64) for which in range(2)]
         for unit in range(2):
             for which in range(2):
                 combine(unit, which, rounded0[which][:, unit * UNIT : (unit + 1) * UNIT, :])
-        wd_rest = work.tile([P, N - WD_SPLIT, PACK], BF16, name="wd_rest", tag=last_wv_tag, align_bytes=64)
+        wd_rest = work.tile([P, N - WD_SPLIT, PACK], BF16, name="wd_rest", tag="q0", align_bytes=64)
         nc.scalar.copy(
             out=wd_rest[:].rearrange("p (g n) i -> p g i n", n=4),
-            in_=wd_raw[1][:].rearrange("p i (g n) -> p g i n", n=4),
+            in_=wd_raw[2][:].rearrange("p i (g n) -> p g i n", n=4),
         )
 
         accs = {}
-        for side in range(2):
+        for side in (VERB, OBJECT):
             for t in range(PACK):
-                accs[side, t] = bank(PACK * side + t, [P, CHUNK])
+                accs[side, t] = bank(PACK * (1 - side) + t, [P, CHUNK])
                 for a in range(PASSES):
                     project(accs[side, t], side, a, t, 1)
-        empty(accs, 0, 1, 0, CHUNK, "q2")
-        empty(accs, 1, 1, 0, UNIT, "p2")
-        empty(accs, 1, 1, UNIT, CHUNK, "p3")
+        empty(accs, VERB, 1, 0, CHUNK, "p2")
+        empty(accs, OBJECT, 1, 0, UNIT, "q2")
+        empty(accs, OBJECT, 1, UNIT, CHUNK, "q3")
 
         operands0 = [quantise(f"chunk0{which}", rounded0[which][:], CHUNK) for which in range(2)]
-        wd_codes = work.tile([P, N], U32, name="wd_codes", tag="p1", align_bytes=64)
+        wd_codes = work.tile([P, N], U32, name="wd_codes", tag="q1", align_bytes=64)
         wd_plane = keep.tile([P, N], U8, name="wd_plane", align_bytes=64)
         wd_parts = (
-            (0, WD_CUT, wd_first[:, 0:WD_CUT, :]),
-            (WD_CUT, WD_SPLIT, wd_first[:, WD_CUT:WD_SPLIT, :]),
+            (0, WD_SPLIT, wd_first[:]),
             (WD_SPLIT, N, wd_rest[:]),
         )
         for lo, hi, values in wd_parts:

@@ -27,7 +27,8 @@ CHUNKS = S // CHUNK
 UNIT = CHUNK // 2
 QUAD = 32
 ROWS = 4
-SCALE_BASE = P - PASSES * 16
+PASS_ROWS = 16
+SCALE_BASE = P - PASSES * PASS_ROWS
 PER_COLUMN = 16
 LAST_TILE = N // P - 1
 SUM, DIFFERENCE = 0, 1
@@ -43,15 +44,17 @@ def tile_list_metaphor_spotting_kernel(
     with ExitStack() as ctx:
         keep = ctx.enter_context(tc.tile_pool(name="keep", bufs=1))
         work = ctx.enter_context(tc.tile_pool(name="work", bufs=1))
+        relay = ctx.enter_context(tc.tile_pool(name="relay", bufs=1))
         psum = ctx.enter_context(tc.psum_pool(name="psum", bufs=1))
 
         def bank(index, shape):
             return psum.tile(shape, F32, name=f"bank{index}", tag=f"bank{index}")
 
-        table_scales = work.tile([P, T], U8, name="table_scales", tag="table_late", align_bytes=64)
+        table_scales = relay.tile([P, T], U8, name="table_scales", offset=0, align_bytes=64)
         nc.vector.memset(table_scales[0:SCALE_BASE, :].bitcast(I32), 0)
-        table_planes = keep.tile([P, PASSES * 2 * S], U8, name="table_planes", align_bytes=64)
-        nc.vector.memset(table_planes[:].bitcast(I32), 0)
+        table_planes = [keep.tile([P, 2 * S], U8, name=f"table_planes{a}", align_bytes=64) for a in range(PASSES)]
+        for planes in table_planes:
+            nc.vector.memset(planes[:].bitcast(I32), 0)
         wo_scales_raw = keep.tile([P, PASSES * H], U8, name="wo_scales_raw", align_bytes=64)
         nc.vector.memset(wo_scales_raw[:].bitcast(I32), 0)
         ws_plane = keep.tile([P, N], U8, name="ws_plane", align_bytes=64)
@@ -60,7 +63,7 @@ def tile_list_metaphor_spotting_kernel(
         lists = [keep.tile([P, S // PER_COLUMN], U16, name=f"list{side}") for side in range(2)]
         nc.sync.dma_start(lists[VERB][:], offs)
         nc.sync.dma_start(
-            out=table_scales[SCALE_BASE:P, :].bitcast(I32), in_=tab_scales.rearrange("a q t -> q a t").bitcast(I32)
+            out=table_scales[SCALE_BASE:P, :].bitcast(I32), in_=tab_scales.rearrange("a q t -> (a q) t").bitcast(I32)
         )
         nc.sync.dma_start(lists[OBJECT][:], offs2)
         table_words = [keep.tile([P, T], U16, name="table_words0", align_bytes=64)]
@@ -80,19 +83,24 @@ def tile_list_metaphor_spotting_kernel(
         wo_raw = [keep.tile([P, H], I32, name="wo_raw0", align_bytes=64)]
         nc.sync.dma_start(out=wo_raw[0][:], in_=wo_words[0].rearrange("p c i -> p (c i)").bitcast(I32))
 
-        picked_scales = work.tile([P, 2 * S], U8, name="picked_scales", tag="wo_late", align_bytes=64)
+        picked_scales = keep.tile([P, 2 * S], U8, name="picked_scales", align_bytes=64)
         for side in (VERB, OBJECT):
             nc.vector.tensor_copy(picked_scales[:, side * S : (side + 1) * S], table_scales[:].indirect(lists[side][:]))
-        for x in range(P // QUAD):
-            first = SCALE_BASE + PASSES * ROWS * x
-            nc.sync.dma_start(
-                out=table_planes[QUAD * x : QUAD * x + ROWS, :].bitcast(I32).rearrange("y (a c) -> y a c", a=PASSES),
-                in_=picked_scales[first : first + PASSES * ROWS, :].bitcast(I32),
-            )
-        table_words.append(work.tile([P, T], U16, name="table_words1", tag="table_late", align_bytes=64))
+
+        def move_planes(a):
+            for y in range(ROWS):
+                first = SCALE_BASE + PASS_ROWS * a + y
+                nc.sync.dma_start(
+                    out=table_planes[a][y:P:QUAD, :].bitcast(I32),
+                    in_=picked_scales[first : first + PASS_ROWS - y : ROWS, :].bitcast(I32),
+                )
+
+        move_planes(0)
+        table_words.append(relay.tile([P, T], U16, name="table_words1", offset=4 * H, align_bytes=64))
         nc.sync.dma_start(out=table_words[1][:].bitcast(I32), in_=tab_words[1].bitcast(I32))
-        wo_raw.append(work.tile([P, H], I32, name="wo_raw1", tag="wo_late", align_bytes=64))
+        wo_raw.append(relay.tile([P, H], I32, name="wo_raw1", offset=0, align_bytes=64))
         nc.sync.dma_start(out=wo_raw[1][:], in_=wo_words[1].rearrange("p c i -> p (c i)").bitcast(I32))
+        move_planes(1)
         biases = []
         for side, bias in enumerate((bo, bv)):
             tile = keep.tile([P, PACK], F32, name=f"bias{side}")
@@ -188,7 +196,7 @@ def tile_list_metaphor_spotting_kernel(
                 lhsT=codes[a][:, cols].bitcast(FP8X4),
                 lhsT_scale=planes[a][:, cols],
                 rhs=picked[side, a, c].bitcast(FP4X4),
-                rhs_scale=table_planes[:, (2 * a + side) * S + c * CHUNK : (2 * a + side) * S + (c + 1) * CHUNK],
+                rhs_scale=table_planes[a][:, side * S + c * CHUNK : side * S + (c + 1) * CHUNK],
                 start=(a == 0),
                 stop=(a == PASSES - 1),
             )

@@ -1,6 +1,7 @@
 from contextlib import ExitStack
 
 import concourse.mybir as mybir
+from concourse.masks import make_identity
 
 K, H, N, T, S = 1024, 512, 640, 4096, 1024
 FLOPS = 2 * S * (2 * K * H + 2 * H * N)
@@ -74,6 +75,8 @@ def tile_list_metaphor_spotting_kernel(
                 out=wo_scales_raw[y:P:QUAD, :].bitcast(I32).rearrange("x (a c) -> x a c", a=PASSES),
                 in_=wo_rows[y].bitcast(I32),
             )
+        identity = keep.tile([P, P], F32, name="identity")
+        make_identity(nc, identity[:])
         wv_raw = []
         for a in range(PASSES):
             tile = keep.tile([P, PACK, H], F32, name=f"wv_raw{a}", align_bytes=64)
@@ -243,7 +246,7 @@ def tile_list_metaphor_spotting_kernel(
             for which in range(2):
                 combine(unit, which, rounded0[which][:, unit * UNIT : (unit + 1) * UNIT, :])
         wd_rest = work.tile([P, N - WD_SPLIT, PACK], BF16, name="wd_rest", tag="q0", align_bytes=64)
-        nc.scalar.copy(
+        nc.vector.tensor_copy(
             out=wd_rest[:].rearrange("p (g n) i -> p g i n", n=4),
             in_=wd_raw[2][:].rearrange("p i (g n) -> p g i n", n=4),
         )
@@ -345,32 +348,55 @@ def tile_list_metaphor_spotting_kernel(
         for n in range(1, LAST_TILE):
             finish_tile(n, tiles0[n])
 
-        combine(3, SUM, rounded1[3][SUM][:])
-        y1_20 = copy_out("y1_20", pair_product(SUM, 0, 2, operands2[SUM]), [P, 2, UNIT])
+        turned = []
+        for j in range(UNIT // P):
+            acc = bank(2 + 2 * j, [P, PACK, P])
+            for t in range(PACK):
+                for side in (VERB, OBJECT):
+                    nc.tensor.matmul(
+                        out=acc[:, t, :],
+                        lhsT=projected[side, 3][:, t, j * P : (j + 1) * P],
+                        rhs=identity[:],
+                        is_transpose=True,
+                        start=(side == VERB),
+                        stop=(side == OBJECT),
+                    )
+            tile = work.tile([P, 2, P, 2], BF16, name=f"turned{j}", align_bytes=64)
+            nc.scalar.copy(out=tile[:], in_=acc[:].rearrange("p (u e) m -> p u m e", e=2))
+            turned.append(tile)
+        back = bank(6, [P, UNIT // P, 2, P])
+        for j, tile in enumerate(turned):
+            words = tile[:].rearrange("p u m e -> p u (m e)").bitcast(F32)
+            for u in range(2):
+                nc.tensor.transpose(back[:, j, u, :], words[:, u, :], identity[:])
+        y1_20 = copy_out("y1_20", pair_product(SUM, 0, 0, operands2[SUM]), [P, 2, UNIT])
+        nc.scalar.copy(
+            out=rounded1[3][SUM][:].bitcast(F32).rearrange("p (j s) u -> p j s u", s=P),
+            in_=back[:].rearrange("p j u s -> p j s u"),
+        )
+
+        combine(3, DIFFERENCE, rounded1[3][DIFFERENCE][:])
         y2_20 = pair_product(DIFFERENCE, 0, 3, operands2[DIFFERENCE])
-        last2 = bank(6, [P, 2, UNIT])
+        y2_21 = pair_product(DIFFERENCE, 1, 5, operands2[DIFFERENCE])
+        finish_tile(LAST_TILE, tiles0[LAST_TILE])
+        differences3 = quantise("unit31", rounded1[3][DIFFERENCE][:], UNIT)
+        sums3 = quantise("unit30", rounded1[3][SUM][:], UNIT)
+        y1_21 = copy_out("y1_21", pair_product(SUM, 1, 2, operands2[SUM]), [P, 2, UNIT])
+        last2 = bank(7, [P, 2, UNIT])
         for which in range(2):
             product(last2[:, which, :], which, LAST_TILE, operands2[which])
         y1_2last = copy_out("y1_2last", last2[:, SUM, :], [P, UNIT])
-        y1_21 = copy_out("y1_21", pair_product(SUM, 1, 4, operands2[SUM]), [P, 2, UNIT])
-        y2_21 = pair_product(DIFFERENCE, 1, 5, operands2[DIFFERENCE])
-
-        finish_tile(LAST_TILE, tiles0[LAST_TILE])
-        sums3 = quantise("unit30", rounded1[3][SUM][:], UNIT)
-        y1_30 = copy_out("y1_30", pair_product(SUM, 0, 0, sums3), [P, 2, UNIT])
-        y1_31 = copy_out("y1_31", pair_product(SUM, 1, 2, sums3), [P, 2, UNIT])
-        last3 = bank(4, [P, 2, UNIT])
-        product(last3[:, SUM, :], SUM, LAST_TILE, sums3)
+        y1_30 = copy_out("y1_30", pair_product(SUM, 0, 4, sums3), [P, 2, UNIT])
+        y2_30 = pair_product(DIFFERENCE, 0, 1, differences3)
+        y1_31 = copy_out("y1_31", pair_product(SUM, 1, 6, sums3), [P, 2, UNIT])
+        last3 = bank(0, [P, 2, UNIT])
+        for which in range(2):
+            product(last3[:, which, :], which, LAST_TILE, (sums3, differences3)[which])
         y1_3last = copy_out("y1_3last", last3[:, SUM, :], [P, UNIT])
-        combine(3, DIFFERENCE, rounded1[3][DIFFERENCE][:])
-        finish_last(2, y1_2last, last2[:, DIFFERENCE, :])
-        differences3 = quantise("unit31", rounded1[3][DIFFERENCE][:], UNIT)
-        y2_30 = pair_product(DIFFERENCE, 0, 7, differences3)
-        y2_31 = pair_product(DIFFERENCE, 1, 1, differences3)
-        product(last3[:, DIFFERENCE, :], DIFFERENCE, LAST_TILE, differences3)
-
         finish_pair(2, 0, y1_20, y2_20)
+        y2_31 = pair_product(DIFFERENCE, 1, 3, differences3)
         finish_pair(2, 1, y1_21, y2_21)
+        finish_last(2, y1_2last, last2[:, DIFFERENCE, :])
         finish_pair(3, 0, y1_30, y2_30)
         finish_pair(3, 1, y1_31, y2_31)
         finish_last(3, y1_3last, last3[:, DIFFERENCE, :])

@@ -245,11 +245,6 @@ def tile_list_metaphor_spotting_kernel(
         for unit in range(2):
             for which in range(2):
                 combine(unit, which, rounded0[which][:, unit * UNIT : (unit + 1) * UNIT, :])
-        wd_rest = work.tile([P, N - WD_SPLIT, PACK], BF16, name="wd_rest", tag="q0", align_bytes=64)
-        nc.vector.tensor_copy(
-            out=wd_rest[:].rearrange("p (g n) i -> p g i n", n=4),
-            in_=wd_raw[2][:].rearrange("p i (g n) -> p g i n", n=4),
-        )
 
         accs = {}
         for side in (VERB, OBJECT):
@@ -264,16 +259,15 @@ def tile_list_metaphor_spotting_kernel(
         operands0 = [quantise(f"chunk0{which}", rounded0[which][:], CHUNK) for which in range(2)]
         wd_codes = work.tile([P, N], U32, name="wd_codes", tag="q1", align_bytes=64)
         wd_plane = keep.tile([P, N], U8, name="wd_plane", align_bytes=64)
-        wd_parts = (
-            (0, WD_SPLIT, wd_first[:]),
-            (WD_SPLIT, N, wd_rest[:]),
-        )
-        for lo, hi, values in wd_parts:
+
+        def quantise_wd(lo, hi, values):
             nc.vector.quantize_mx(
                 out=wd_codes[:, lo:hi].bitcast(FP8X4),
                 scales=wd_plane[:, lo:hi],
                 in_=values.rearrange("p n i -> p (n i)"),
             )
+
+        quantise_wd(0, WD_SPLIT, wd_first[:])
 
         def product(acc, which, n, operand):
             rows = slice(n * P, (n + 1) * P)
@@ -301,14 +295,15 @@ def tile_list_metaphor_spotting_kernel(
             nc.vector.tensor_tensor(out=result[:], in0=y2, in1=y1_copy[:], op=MULT)
             nc.sync.dma_start(out=dest, in_=result[:])
 
-        def tile_products(n):
-            index = 2 * n % 8
-            y1 = bank(index, [P, CHUNK])
+        def first_product(n):
+            y1 = bank(2 * n % 8, [P, CHUNK])
             product(y1[:], SUM, n, operands0[SUM])
-            y1_copy = copy_out(f"y1_0{n}", y1[:], [P, CHUNK])
-            y2 = bank(index + 1, [P, CHUNK])
+            return copy_out(f"y1_0{n}", y1[:], [P, CHUNK])
+
+        def second_product(n):
+            y2 = bank((2 * n + 1) % 8, [P, CHUNK])
             product(y2[:], DIFFERENCE, n, operands0[DIFFERENCE])
-            return y1_copy, y2[:]
+            return y2[:]
 
         def finish_tile(n, made):
             multiply(f"0{n}", made[0], made[1], [P, CHUNK], out[n * P : (n + 1) * P, 0:CHUNK])
@@ -334,18 +329,21 @@ def tile_list_metaphor_spotting_kernel(
             ]
             for unit in (2, 3)
         }
-        y1_00, y2_00 = tile_products(0)
         for which in range(2):
             combine(2, which, rounded1[2][which][:])
         operands2 = [quantise(f"unit2{which}", rounded1[2][which][:], UNIT) for which in range(2)]
 
-        y2_00_copy = copy_out("y2_00", y2_00, [P, CHUNK])
-        result_00 = work.tile([P, CHUNK], F32, name="result_00", tag="rounded21", align_bytes=64)
-        nc.gpsimd.tensor_tensor(out=result_00[:], in0=y2_00_copy[:], in1=y1_00[:], op=MULT)
-        nc.sync.dma_start(out=out[0:P, 0:CHUNK], in_=result_00[:])
-
-        tiles0 = {n: tile_products(n) for n in range(1, LAST_TILE + 1)}
-        for n in range(1, LAST_TILE):
+        wd_rest = work.tile([P, N - WD_SPLIT, PACK], BF16, name="wd_rest", tag="rounded21", align_bytes=64)
+        nc.gpsimd.tensor_scalar(
+            out=wd_rest[:],
+            in0=wd_raw[2][:].rearrange("p i n -> p n i"),
+            scalar1=1.0,
+            scalar2=0.0,
+            op0=MULT,
+            op1=ADD,
+        )
+        tiles0 = {n: (first_product(n), second_product(n)) for n in range(LAST_TILE)}
+        for n in range(LAST_TILE):
             finish_tile(n, tiles0[n])
 
         turned = []
@@ -369,34 +367,38 @@ def tile_list_metaphor_spotting_kernel(
             words = tile[:].rearrange("p u m e -> p u (m e)").bitcast(F32)
             for u in range(2):
                 nc.tensor.transpose(back[:, j, u, :], words[:, u, :], identity[:])
-        y1_20 = copy_out("y1_20", pair_product(SUM, 0, 0, operands2[SUM]), [P, 2, UNIT])
+        y1_04 = first_product(LAST_TILE)
         nc.scalar.copy(
             out=rounded1[3][SUM][:].bitcast(F32).rearrange("p (j s) u -> p j s u", s=P),
             in_=back[:].rearrange("p j u s -> p j s u"),
         )
 
-        combine(3, DIFFERENCE, rounded1[3][DIFFERENCE][:])
-        y2_20 = pair_product(DIFFERENCE, 0, 3, operands2[DIFFERENCE])
-        y2_21 = pair_product(DIFFERENCE, 1, 5, operands2[DIFFERENCE])
-        finish_tile(LAST_TILE, tiles0[LAST_TILE])
-        differences3 = quantise("unit31", rounded1[3][DIFFERENCE][:], UNIT)
-        sums3 = quantise("unit30", rounded1[3][SUM][:], UNIT)
-        y1_21 = copy_out("y1_21", pair_product(SUM, 1, 2, operands2[SUM]), [P, 2, UNIT])
+        quantise_wd(WD_SPLIT, N, wd_rest[:])
+        y2_04 = second_product(LAST_TILE)
         last2 = bank(7, [P, 2, UNIT])
         for which in range(2):
             product(last2[:, which, :], which, LAST_TILE, operands2[which])
         y1_2last = copy_out("y1_2last", last2[:, SUM, :], [P, UNIT])
-        y1_30 = copy_out("y1_30", pair_product(SUM, 0, 4, sums3), [P, 2, UNIT])
-        y2_30 = pair_product(DIFFERENCE, 0, 1, differences3)
-        y1_31 = copy_out("y1_31", pair_product(SUM, 1, 6, sums3), [P, 2, UNIT])
-        last3 = bank(0, [P, 2, UNIT])
-        for which in range(2):
-            product(last3[:, which, :], which, LAST_TILE, (sums3, differences3)[which])
+        y1_20 = copy_out("y1_20", pair_product(SUM, 0, 2, operands2[SUM]), [P, 2, UNIT])
+        y1_21 = copy_out("y1_21", pair_product(SUM, 1, 4, operands2[SUM]), [P, 2, UNIT])
+        y2_20 = pair_product(DIFFERENCE, 0, 3, operands2[DIFFERENCE])
+        y2_21 = pair_product(DIFFERENCE, 1, 5, operands2[DIFFERENCE])
+        combine(3, DIFFERENCE, rounded1[3][DIFFERENCE][:])
+        sums3 = quantise("unit30", rounded1[3][SUM][:], UNIT)
+        y1_30 = copy_out("y1_30", pair_product(SUM, 0, 6, sums3), [P, 2, UNIT])
+        y1_31 = copy_out("y1_31", pair_product(SUM, 1, 0, sums3), [P, 2, UNIT])
+        last3 = bank(2, [P, 2, UNIT])
+        product(last3[:, SUM, :], SUM, LAST_TILE, sums3)
         y1_3last = copy_out("y1_3last", last3[:, SUM, :], [P, UNIT])
-        finish_pair(2, 0, y1_20, y2_20)
-        y2_31 = pair_product(DIFFERENCE, 1, 3, differences3)
-        finish_pair(2, 1, y1_21, y2_21)
+        finish_tile(LAST_TILE, (y1_04, y2_04))
         finish_last(2, y1_2last, last2[:, DIFFERENCE, :])
+        differences3 = quantise("unit31", rounded1[3][DIFFERENCE][:], UNIT)
+        y2_30 = pair_product(DIFFERENCE, 0, 1, differences3)
+        y2_31 = pair_product(DIFFERENCE, 1, 7, differences3)
+        product(last3[:, DIFFERENCE, :], DIFFERENCE, LAST_TILE, differences3)
+
+        finish_pair(2, 0, y1_20, y2_20)
+        finish_pair(2, 1, y1_21, y2_21)
         finish_pair(3, 0, y1_30, y2_30)
         finish_pair(3, 1, y1_31, y2_31)
         finish_last(3, y1_3last, last3[:, DIFFERENCE, :])

@@ -33,9 +33,12 @@ SCALE_BASE = P - PASSES * PASS_ROWS
 PER_COLUMN = 16
 LAST_TILE = N // P - 1
 SUM, DIFFERENCE = 0, 1
-WD_SPLIT = 512
+WD_SPLIT = 384
 WD_PIECES = ((0, 256), (256, WD_SPLIT), (WD_SPLIT, N))
 VERB, OBJECT = 1, 0
+Y1_BANKS = (0, 2, 4, 0, 2)
+Y2_BANKS = (1, 3, 5, 7, 1)
+EARLY_TILES = WD_SPLIT // P
 
 
 def tile_list_metaphor_spotting_kernel(
@@ -86,6 +89,14 @@ def tile_list_metaphor_spotting_kernel(
         wo_raw = [keep.tile([P, H], I32, name="wo_raw0", align_bytes=64)]
         nc.sync.dma_start(out=wo_raw[0][:], in_=wo_words[0].rearrange("p c i -> p (c i)").bitcast(I32))
 
+        biases = {}
+
+        def load_bias(side, bias):
+            biases[side] = keep.tile([P, PACK], F32, name=f"bias{side}")
+            nc.sync.dma_start(out=biases[side][:], in_=bias.rearrange("(m t) -> m t", t=PACK))
+
+        load_bias(OBJECT, bo)
+
         picked_scales = keep.tile([P, 2 * S], U8, name="picked_scales", align_bytes=64)
         for side in (VERB, OBJECT):
             nc.vector.tensor_copy(picked_scales[:, side * S : (side + 1) * S], table_scales[:].indirect(lists[side][:]))
@@ -104,11 +115,7 @@ def tile_list_metaphor_spotting_kernel(
         wo_raw.append(relay.tile([P, H], I32, name="wo_raw1", offset=0, align_bytes=64))
         nc.sync.dma_start(out=wo_raw[1][:], in_=wo_words[1].rearrange("p c i -> p (c i)").bitcast(I32))
         move_planes(1)
-        biases = []
-        for side, bias in enumerate((bo, bv)):
-            tile = keep.tile([P, PACK], F32, name=f"bias{side}")
-            nc.sync.dma_start(out=tile[:], in_=bias.rearrange("(m t) -> m t", t=PACK))
-            biases.append(tile)
+        load_bias(VERB, bv)
 
         wd_raw = []
         for lo, hi in WD_PIECES:
@@ -296,12 +303,12 @@ def tile_list_metaphor_spotting_kernel(
             nc.sync.dma_start(out=dest, in_=result[:])
 
         def first_product(n):
-            y1 = bank(2 * n % 8, [P, CHUNK])
+            y1 = bank(Y1_BANKS[n], [P, CHUNK])
             product(y1[:], SUM, n, operands0[SUM])
             return copy_out(f"y1_0{n}", y1[:], [P, CHUNK])
 
         def second_product(n):
-            y2 = bank((2 * n + 1) % 8, [P, CHUNK])
+            y2 = bank(Y2_BANKS[n], [P, CHUNK])
             product(y2[:], DIFFERENCE, n, operands0[DIFFERENCE])
             return y2[:]
 
@@ -342,9 +349,13 @@ def tile_list_metaphor_spotting_kernel(
             op0=MULT,
             op1=ADD,
         )
-        tiles0 = {n: (first_product(n), second_product(n)) for n in range(LAST_TILE)}
-        for n in range(LAST_TILE):
+        tiles0 = {n: (first_product(n), second_product(n)) for n in range(EARLY_TILES)}
+        y1_03 = first_product(EARLY_TILES)
+        y1_20 = copy_out("y1_20", pair_product(SUM, 0, 6, operands2[SUM]), [P, 2, UNIT])
+        y2_20 = pair_product(DIFFERENCE, 0, 7, operands2[DIFFERENCE])
+        for n in range(EARLY_TILES):
             finish_tile(n, tiles0[n])
+        finish_pair(2, 0, y1_20, y2_20)
 
         turned = []
         for j in range(UNIT // P):
@@ -374,31 +385,30 @@ def tile_list_metaphor_spotting_kernel(
         )
 
         quantise_wd(WD_SPLIT, N, wd_rest[:])
-        y2_04 = second_product(LAST_TILE)
-        last2 = bank(7, [P, 2, UNIT])
+        y2_03 = second_product(EARLY_TILES)
+        last2 = bank(3, [P, 2, UNIT])
         for which in range(2):
             product(last2[:, which, :], which, LAST_TILE, operands2[which])
         y1_2last = copy_out("y1_2last", last2[:, SUM, :], [P, UNIT])
-        y1_20 = copy_out("y1_20", pair_product(SUM, 0, 2, operands2[SUM]), [P, 2, UNIT])
+        y2_04 = second_product(LAST_TILE)
         y1_21 = copy_out("y1_21", pair_product(SUM, 1, 4, operands2[SUM]), [P, 2, UNIT])
-        y2_20 = pair_product(DIFFERENCE, 0, 3, operands2[DIFFERENCE])
         y2_21 = pair_product(DIFFERENCE, 1, 5, operands2[DIFFERENCE])
         combine(3, DIFFERENCE, rounded1[3][DIFFERENCE][:])
+        finish_tile(EARLY_TILES, (y1_03, y2_03))
         sums3 = quantise("unit30", rounded1[3][SUM][:], UNIT)
         y1_30 = copy_out("y1_30", pair_product(SUM, 0, 6, sums3), [P, 2, UNIT])
         y1_31 = copy_out("y1_31", pair_product(SUM, 1, 0, sums3), [P, 2, UNIT])
-        last3 = bank(2, [P, 2, UNIT])
-        product(last3[:, SUM, :], SUM, LAST_TILE, sums3)
-        y1_3last = copy_out("y1_3last", last3[:, SUM, :], [P, UNIT])
-        finish_tile(LAST_TILE, (y1_04, y2_04))
+        last3 = [bank(index, [P, UNIT]) for index in (2, 4)]
+        product(last3[SUM][:], SUM, LAST_TILE, sums3)
+        y1_3last = copy_out("y1_3last", last3[SUM][:], [P, UNIT])
         finish_last(2, y1_2last, last2[:, DIFFERENCE, :])
         differences3 = quantise("unit31", rounded1[3][DIFFERENCE][:], UNIT)
-        y2_30 = pair_product(DIFFERENCE, 0, 1, differences3)
-        y2_31 = pair_product(DIFFERENCE, 1, 7, differences3)
-        product(last3[:, DIFFERENCE, :], DIFFERENCE, LAST_TILE, differences3)
+        y2_30 = pair_product(DIFFERENCE, 0, 7, differences3)
+        y2_31 = pair_product(DIFFERENCE, 1, 3, differences3)
+        product(last3[DIFFERENCE][:], DIFFERENCE, LAST_TILE, differences3)
 
-        finish_pair(2, 0, y1_20, y2_20)
+        finish_tile(LAST_TILE, (y1_04, y2_04))
         finish_pair(2, 1, y1_21, y2_21)
         finish_pair(3, 0, y1_30, y2_30)
         finish_pair(3, 1, y1_31, y2_31)
-        finish_last(3, y1_3last, last3[:, DIFFERENCE, :])
+        finish_last(3, y1_3last, last3[DIFFERENCE][:])

@@ -82,7 +82,7 @@ def tile_list_metaphor_spotting_kernel(
         make_identity(nc, identity[:])
         wv_raw = []
         for a in range(PASSES):
-            tile = keep.tile([P, PACK, H], F32, name=f"wv_raw{a}", align_bytes=64)
+            tile = work.tile([P, PACK, H], F32, name=f"wv_raw{a}", tag=f"wv_raw{a}", align_bytes=64)
             rows = wv[a * K_PASS : (a + 1) * K_PASS, :]
             nc.sync.dma_start(out=tile[:], in_=rows.rearrange("(p i) c -> p i c", i=PACK))
             wv_raw.append(tile)
@@ -166,7 +166,7 @@ def tile_list_metaphor_spotting_kernel(
             wv_codes.append(codes)
             wv_planes.append(plane)
             if a == 0:
-                objects_rest = work.tile([P, CHUNK], U16, name="objects_rest", tag="wv_rounded0", align_bytes=64)
+                objects_rest = work.tile([P, CHUNK], U16, name="objects_rest", tag="wv_raw0", align_bytes=64)
                 gather_chunk(objects_rest[:], OBJECT, 0, 1)
 
         wo_codes = []
@@ -178,7 +178,7 @@ def tile_list_metaphor_spotting_kernel(
             )
             wo_codes.append(codes)
 
-        picked_second = work.tile([P, 2 * S], U16, name="picked_second", tag="wv_rounded1", align_bytes=64)
+        picked_second = work.tile([P, 2 * S], U16, name="picked_second", tag="wv_raw1", align_bytes=64)
         for c in range(CHUNKS):
             for place, side in enumerate((VERB, OBJECT)):
                 lo = (2 * c + place) * CHUNK

@@ -56,11 +56,11 @@ def tile_list_metaphor_spotting_kernel(
 
         table_scales = relay.tile([P, T], U8, name="table_scales", offset=0, align_bytes=64)
         nc.vector.memset(table_scales[0:SCALE_BASE, :].bitcast(I32), 0)
+        wo_scales_raw = keep.tile([P, PASSES * H], U8, name="wo_scales_raw", align_bytes=64)
+        nc.vector.memset(wo_scales_raw[:].bitcast(I32), 0)
         table_planes = [keep.tile([P, 2 * S], U8, name=f"table_planes{a}", align_bytes=64) for a in range(PASSES)]
         for planes in table_planes:
             nc.vector.memset(planes[:].bitcast(I32), 0)
-        wo_scales_raw = keep.tile([P, PASSES * H], U8, name="wo_scales_raw", align_bytes=64)
-        nc.vector.memset(wo_scales_raw[:].bitcast(I32), 0)
         ws_plane = keep.tile([P, N], U8, name="ws_plane", align_bytes=64)
         nc.vector.memset(ws_plane[:].bitcast(I32), 0)
 
@@ -74,7 +74,7 @@ def tile_list_metaphor_spotting_kernel(
         nc.sync.dma_start(out=table_words[0][:].bitcast(I32), in_=tab_words[0].bitcast(I32))
         wo_rows = wo_scales.rearrange("a (x y) c -> y x a c", y=ROWS)
         for y in range(ROWS):
-            nc.gpsimd.dma_start(
+            nc.sync.dma_start(
                 out=wo_scales_raw[y:P:QUAD, :].bitcast(I32).rearrange("x (a c) -> x a c", a=PASSES),
                 in_=wo_rows[y].bitcast(I32),
             )

from contextlib import ExitStack

import concourse.mybir as mybir
from concourse.masks import make_identity

K, H, N, T, S = 1024, 512, 640, 4096, 1024
FLOPS = 2 * S * (2 * K * H + 2 * H * N)

F32 = mybir.dt.float32
BF16 = mybir.dt.bfloat16
I32 = mybir.dt.int32
U32 = mybir.dt.uint32
U16 = mybir.dt.uint16
U8 = mybir.dt.uint8
FP8X4 = mybir.dt.float8_e4m3fn_x4
FP4X4 = mybir.dt.float4_e2m1fn_x4
IDENTITY = mybir.ActivationFunctionType.Identity
ADD = mybir.AluOpType.add
SUBTRACT = mybir.AluOpType.subtract
MULT = mybir.AluOpType.mult

P = 128
PACK = 4
K_PASS = P * PACK
PASSES = K // K_PASS
CHUNK = 512
CHUNKS = S // CHUNK
UNIT = CHUNK // 2
QUAD = 32
ROWS = 4
PASS_ROWS = 16
SCALE_BASE = P - PASSES * PASS_ROWS
PER_COLUMN = 16
LAST_TILE = N // P - 1
SUM, DIFFERENCE = 0, 1
WD_SPLIT = 384
WD_PIECES = ((0, 256), (256, WD_SPLIT), (WD_SPLIT, N))
VERB, OBJECT = 1, 0
Y1_BANKS = (0, 2, 4, 0, 2)
Y2_BANKS = (1, 3, 5, 7, 1)
EARLY_TILES = WD_SPLIT // P


def tile_list_metaphor_spotting_kernel(
    tc, tab_words, tab_scales, offs, offs2, wv, wo_words, wo_scales, bv, bo, ws_words, ws_scales, wd, out
):
    nc = tc.nc
    with ExitStack() as ctx:
        keep = ctx.enter_context(tc.tile_pool(name="keep", bufs=1))
        work = ctx.enter_context(tc.tile_pool(name="work", bufs=1))
        relay = ctx.enter_context(tc.tile_pool(name="relay", bufs=1))
        psum = ctx.enter_context(tc.psum_pool(name="psum", bufs=1))

        def bank(index, shape):
            return psum.tile(shape, F32, name=f"bank{index}", tag=f"bank{index}")

        table_scales = relay.tile([P, T], U8, name="table_scales", offset=0, align_bytes=64)
        nc.vector.memset(table_scales[0:SCALE_BASE, :].bitcast(I32), 0)
        wo_scales_raw = keep.tile([P, PASSES * H], U8, name="wo_scales_raw", align_bytes=64)
        nc.vector.memset(wo_scales_raw[:].bitcast(I32), 0)
        table_planes = [keep.tile([P, 2 * S], U8, name=f"table_planes{a}", align_bytes=64) for a in range(PASSES)]
        for planes in table_planes:
            nc.vector.memset(planes[:].bitcast(I32), 0)
        ws_plane = keep.tile([P, N], U8, name="ws_plane", align_bytes=64)
        nc.vector.memset(ws_plane[:].bitcast(I32), 0)

        lists = [keep.tile([P, S // PER_COLUMN], U16, name=f"list{side}") for side in range(2)]
        nc.sync.dma_start(lists[VERB][:], offs)
        nc.sync.dma_start(
            out=table_scales[SCALE_BASE:P, :].bitcast(I32), in_=tab_scales.rearrange("a q t -> (a q) t").bitcast(I32)
        )
        nc.sync.dma_start(lists[OBJECT][:], offs2)
        table_words = [keep.tile([P, T], U16, name="table_words0", align_bytes=64)]
        nc.sync.dma_start(out=table_words[0][:].bitcast(I32), in_=tab_words[0].bitcast(I32))
        wo_rows = wo_scales.rearrange("a (x y) c -> y x a c", y=ROWS)
        for y in range(ROWS):
            nc.sync.dma_start(
                out=wo_scales_raw[y:P:QUAD, :].bitcast(I32).rearrange("x (a c) -> x a c", a=PASSES),
                in_=wo_rows[y].bitcast(I32),
            )
        identity = keep.tile([P, P], F32, name="identity")
        make_identity(nc, identity[:])
        wv_raw = []
        for a in range(PASSES):
            tile = work.tile([P, PACK, H], F32, name=f"wv_raw{a}", tag=f"wv_raw{a}", align_bytes=64)
            rows = wv[a * K_PASS : (a + 1) * K_PASS, :]
            nc.sync.dma_start(out=tile[:], in_=rows.rearrange("(p i) c -> p i c", i=PACK))
            wv_raw.append(tile)
        wo_raw = [keep.tile([P, H], I32, name="wo_raw0", align_bytes=64)]
        nc.sync.dma_start(out=wo_raw[0][:], in_=wo_words[0].rearrange("p c i -> p (c i)").bitcast(I32))

        biases = {}

        def load_bias(side, bias):
            biases[side] = keep.tile([P, PACK], F32, name=f"bias{side}")
            nc.sync.dma_start(out=biases[side][:], in_=bias.rearrange("(m t) -> m t", t=PACK))

        load_bias(OBJECT, bo)

        picked_scales = keep.tile([P, 2 * S], U8, name="picked_scales", align_bytes=64)
        for side in (VERB, OBJECT):
            nc.vector.tensor_copy(picked_scales[:, side * S : (side + 1) * S], table_scales[:].indirect(lists[side][:]))

        def move_planes(a):
            for y in range(ROWS):
                first = SCALE_BASE + PASS_ROWS * a + y
                nc.sync.dma_start(
                    out=table_planes[a][y:P:QUAD, :].bitcast(I32),
                    in_=picked_scales[first : first + PASS_ROWS - y : ROWS, :].bitcast(I32),
                )

        move_planes(0)
        table_words.append(relay.tile([P, T], U16, name="table_words1", offset=4 * H, align_bytes=64))
        nc.sync.dma_start(out=table_words[1][:].bitcast(I32), in_=tab_words[1].bitcast(I32))
        wo_raw.append(relay.tile([P, H], I32, name="wo_raw1", offset=0, align_bytes=64))
        nc.sync.dma_start(out=wo_raw[1][:], in_=wo_words[1].rearrange("p c i -> p (c i)").bitcast(I32))
        move_planes(1)
        load_bias(VERB, bv)

        wd_raw = []
        for lo, hi in WD_PIECES:
            tile = keep.tile([P, PACK, hi - lo], F32, name=f"wd_raw{lo}")
            nc.sync.dma_start(out=tile[:], in_=wd[:, lo:hi].rearrange("(p i) n -> p i n", i=PACK))
            wd_raw.append(tile)
        ws_codes = keep.tile([P, 2 * N], U8, name="ws_codes", align_bytes=64)
        nc.sync.dma_start(out=ws_codes[:].bitcast(I32), in_=ws_words[0].bitcast(I32))
        ws_rows = ws_scales[0].rearrange("(x y) n -> y x n", y=ROWS)
        for y in range(ROWS):
            nc.sync.dma_start(out=ws_plane[y:P:QUAD, :].bitcast(I32), in_=ws_rows[y].bitcast(I32))

        wo_planes = []
        for a in range(PASSES):
            plane = keep.tile([P, H], U8, name=f"wo_plane{a}", align_bytes=64)
            nc.gpsimd.tensor_copy(
                out=plane[:].rearrange("p (t m) -> p t m", t=PACK),
                in_=wo_scales_raw[:, a * H : (a + 1) * H].rearrange("p (m t) -> p t m", t=PACK),
            )
            wo_planes.append(plane)

        picked = {}
        columns = CHUNK // PER_COLUMN

        def gather_chunk(dest, side, a, c):
            nc.vector.tensor_copy(dest, table_words[a][:].indirect(lists[side][:, c * columns : (c + 1) * columns]))
            picked[side, a, c] = dest

        verbs_first = keep.tile([P, S], U16, name="verbs_first", align_bytes=64)
        nc.vector.tensor_copy(verbs_first[:], table_words[0][:].indirect(lists[VERB][:]))
        for c in range(CHUNKS):
            picked[VERB, 0, c] = verbs_first[:, c * CHUNK : (c + 1) * CHUNK]
        objects_first = keep.tile([P, CHUNK], U16, name="objects_first", align_bytes=64)
        gather_chunk(objects_first[:], OBJECT, 0, 0)

        wv_codes, wv_planes = [], []
        for a in range(PASSES):
            wv_rounded = work.tile([P, PACK, P, PACK], BF16, name=f"wv_rounded{a}", tag=f"wv_rounded{a}", align_bytes=64)
            nc.scalar.copy(
                out=wv_rounded[:].rearrange("p t m i -> p m i t"),
                in_=wv_raw[a][:].rearrange("p i (m t) -> p m i t", t=PACK),
            )
            codes = keep.tile([P, H], U32, name=f"wv_codes{a}", align_bytes=64)
            plane = keep.tile([P, H], U8, name=f"wv_plane{a}", align_bytes=64)
            nc.vector.quantize_mx(
                out=codes[:].bitcast(FP8X4), scales=plane[:], in_=wv_rounded[:].rearrange("p t m i -> p (t m i)")
            )
            wv_codes.append(codes)
            wv_planes.append(plane)
            if a == 0:
                objects_rest = work.tile([P, CHUNK], U16, name="objects_rest", tag="wv_raw0", align_bytes=64)
                gather_chunk(objects_rest[:], OBJECT, 0, 1)

        wo_codes = []
        for a in range(PASSES):
            codes = keep.tile([P, H], U32, name=f"wo_codes{a}", align_bytes=64)
            nc.scalar.copy(
                out=codes[:].rearrange("p (t m) -> p m t", t=PACK),
                in_=wo_raw[a][:].bitcast(U32).rearrange("p (m t) -> p m t", t=PACK),
            )
            wo_codes.append(codes)

        picked_second = work.tile([P, 2 * S], U16, name="picked_second", tag="wv_raw1", align_bytes=64)
        for c in range(CHUNKS):
            for place, side in enumerate((VERB, OBJECT)):
                lo = (2 * c + place) * CHUNK
                gather_chunk(picked_second[:, lo : lo + CHUNK], side, 1, c)

        wd_first = keep.tile([P, WD_SPLIT, PACK], BF16, name="wd_first", align_bytes=64)
        for piece in range(2):
            lo, hi = WD_PIECES[piece]
            nc.gpsimd.tensor_scalar(
                out=wd_first[:, lo:hi, :],
                in0=wd_raw[piece][:].rearrange("p i n -> p n i"),
                scalar1=1.0,
                scalar2=0.0,
                op0=MULT,
                op1=ADD,
            )

        first_weights = ((wo_codes, wo_planes), (wv_codes, wv_planes))

        def project(acc, side, a, t, c):
            codes, planes = first_weights[side]
            cols = slice(t * P, (t + 1) * P)
            nc.tensor.matmul_mx(
                out=acc[:],
                lhsT=codes[a][:, cols].bitcast(FP8X4),
                lhsT_scale=planes[a][:, cols],
                rhs=picked[side, a, c].bitcast(FP4X4),
                rhs_scale=table_planes[a][:, side * S + c * CHUNK : side * S + (c + 1) * CHUNK],
                start=(a == 0),
                stop=(a == PASSES - 1),
            )

        projected = {}

        def empty(accs, side, c, lo, hi, tag):
            tile = work.tile([P, PACK, hi - lo], F32, name=f"projected{side}{c}{lo}", tag=tag, align_bytes=64)
            for t in range(PACK):
                nc.scalar.activation(
                    out=tile[:, t, :], in_=accs[side, t][:, lo:hi], func=IDENTITY, bias=biases[side][:, t : t + 1]
                )
            for half in range(lo // UNIT, hi // UNIT):
                projected[side, 2 * c + half] = tile[:, :, half * UNIT - lo : (half + 1) * UNIT - lo]

        def combine(unit, which, dest):
            nc.vector.tensor_tensor(
                out=dest.rearrange("p (g j) t -> p g t j", j=2),
                in0=projected[1, unit].rearrange("p t (g j) -> p g t j", j=2),
                in1=projected[0, unit].rearrange("p t (g j) -> p g t j", j=2),
                op=(ADD, SUBTRACT)[which],
            )

        def quantise(name, values, tokens):
            codes = work.tile([P, tokens], U32, name=f"{name}_codes", align_bytes=64)
            plane = work.tile([P, tokens], U8, name=f"{name}_plane", align_bytes=64)
            nc.vector.quantize_mx(out=codes[:].bitcast(FP8X4), scales=plane[:], in_=values.rearrange("p j t -> p (j t)"))
            return codes, plane

        accs = {}
        for a in range(PASSES):
            for side in (VERB, OBJECT):
                for t in range(PACK):
                    if a == 0:
                        accs[side, t] = bank(PACK * (1 - side) + t, [P, CHUNK])
                    project(accs[side, t], side, a, t, 0)
        empty(accs, VERB, 0, 0, UNIT, "p0")
        empty(accs, OBJECT, 0, 0, UNIT, "q0")
        empty(accs, VERB, 0, UNIT, CHUNK, "p1")
        empty(accs, OBJECT, 0, UNIT, CHUNK, "q1")

        rounded0 = [work.tile([P, CHUNK, PACK], BF16, name=f"rounded0{which}", align_bytes=64) for which in range(2)]
        for unit in range(2):
            for which in range(2):
                combine(unit, which, rounded0[which][:, unit * UNIT : (unit + 1) * UNIT, :])

        accs = {}
        for side in (VERB, OBJECT):
            for t in range(PACK):
                accs[side, t] = bank(PACK * (1 - side) + t, [P, CHUNK])
                for a in range(PASSES):
                    project(accs[side, t], side, a, t, 1)
        empty(accs, VERB, 1, 0, CHUNK, "p2")
        empty(accs, OBJECT, 1, 0, UNIT, "q2")
        empty(accs, OBJECT, 1, UNIT, CHUNK, "q3")

        operands0 = [quantise(f"chunk0{which}", rounded0[which][:], CHUNK) for which in range(2)]
        wd_codes = work.tile([P, N], U32, name="wd_codes", tag="q1", align_bytes=64)
        wd_plane = keep.tile([P, N], U8, name="wd_plane", align_bytes=64)

        def quantise_wd(lo, hi, values):
            nc.vector.quantize_mx(
                out=wd_codes[:, lo:hi].bitcast(FP8X4),
                scales=wd_plane[:, lo:hi],
                in_=values.rearrange("p n i -> p (n i)"),
            )

        quantise_wd(0, WD_SPLIT, wd_first[:])

        def product(acc, which, n, operand):
            rows = slice(n * P, (n + 1) * P)
            if which == SUM:
                codes, plane = ws_codes[:, 2 * n * P : 2 * (n + 1) * P].bitcast(FP4X4), ws_plane[:, rows]
            else:
                codes, plane = wd_codes[:, rows].bitcast(FP8X4), wd_plane[:, rows]
            nc.tensor.matmul_mx(
                out=acc,
                lhsT=codes,
                lhsT_scale=plane,
                rhs=operand[0][:].bitcast(FP8X4),
                rhs_scale=operand[1][:],
                start=True,
                stop=True,
            )

        def copy_out(name, acc, shape):
            tile = work.tile(shape, F32, name=f"copy_{name}")
            nc.scalar.copy(out=tile[:], in_=acc)
            return tile

        def multiply(name, y1_copy, y2, shape, dest):
            result = work.tile(shape, F32, name=f"result_{name}")
            nc.vector.tensor_tensor(out=result[:], in0=y2, in1=y1_copy[:], op=MULT)
            nc.sync.dma_start(out=dest, in_=result[:])

        def first_product(n):
            y1 = bank(Y1_BANKS[n], [P, CHUNK])
            product(y1[:], SUM, n, operands0[SUM])
            return copy_out(f"y1_0{n}", y1[:], [P, CHUNK])

        def second_product(n):
            y2 = bank(Y2_BANKS[n], [P, CHUNK])
            product(y2[:], DIFFERENCE, n, operands0[DIFFERENCE])
            return y2[:]

        def finish_tile(n, made):
            multiply(f"0{n}", made[0], made[1], [P, CHUNK], out[n * P : (n + 1) * P, 0:CHUNK])

        def pair_product(which, pair, index, operand):
            acc = bank(index, [P, 2, UNIT])
            for i in range(2):
                product(acc[:, i, :], which, 2 * pair + i, operand)
            return acc[:]

        def finish_pair(unit, pair, y1_copy, y2):
            dest = out[2 * pair * P : 2 * (pair + 1) * P, unit * UNIT : (unit + 1) * UNIT]
            multiply(f"{unit}{pair}", y1_copy, y2, [P, 2, UNIT], dest.rearrange("(i p) j -> p i j", p=P))

        def finish_last(unit, y1_copy, y2):
            dest = out[LAST_TILE * P : N, unit * UNIT : (unit + 1) * UNIT]
            multiply(f"{unit}last", y1_copy, y2, [P, UNIT], dest)

        rounded1 = {
            unit: [
                work.tile([P, UNIT, PACK], BF16, name=f"rounded{unit}{w}", tag=f"rounded{unit}{w}", align_bytes=64)
                for w in range(2)
            ]
            for unit in (2, 3)
        }
        for which in range(2):
            combine(2, which, rounded1[2][which][:])
        operands2 = [quantise(f"unit2{which}", rounded1[2][which][:], UNIT) for which in range(2)]

        wd_rest = work.tile([P, N - WD_SPLIT, PACK], BF16, name="wd_rest", tag="rounded21", align_bytes=64)
        nc.gpsimd.tensor_scalar(
            out=wd_rest[:],
            in0=wd_raw[2][:].rearrange("p i n -> p n i"),
            scalar1=1.0,
            scalar2=0.0,
            op0=MULT,
            op1=ADD,
        )
        tiles0 = {n: (first_product(n), second_product(n)) for n in range(EARLY_TILES)}
        y1_03 = first_product(EARLY_TILES)
        y1_20 = copy_out("y1_20", pair_product(SUM, 0, 6, operands2[SUM]), [P, 2, UNIT])
        y2_20 = pair_product(DIFFERENCE, 0, 7, operands2[DIFFERENCE])
        for n in range(EARLY_TILES):
            finish_tile(n, tiles0[n])
        finish_pair(2, 0, y1_20, y2_20)

        turned = []
        for j in range(UNIT // P):
            acc = bank(2 + 2 * j, [P, PACK, P])
            for t in range(PACK):
                for side in (VERB, OBJECT):
                    nc.tensor.matmul(
                        out=acc[:, t, :],
                        lhsT=projected[side, 3][:, t, j * P : (j + 1) * P],
                        rhs=identity[:],
                        is_transpose=True,
                        start=(side == VERB),
                        stop=(side == OBJECT),
                    )
            tile = work.tile([P, 2, P, 2], BF16, name=f"turned{j}", align_bytes=64)
            nc.scalar.copy(out=tile[:], in_=acc[:].rearrange("p (u e) m -> p u m e", e=2))
            turned.append(tile)
        back = bank(6, [P, UNIT // P, 2, P])
        for j, tile in enumerate(turned):
            words = tile[:].rearrange("p u m e -> p u (m e)").bitcast(F32)
            for u in range(2):
                nc.tensor.transpose(back[:, j, u, :], words[:, u, :], identity[:])
        y1_04 = first_product(LAST_TILE)
        nc.scalar.copy(
            out=rounded1[3][SUM][:].bitcast(F32).rearrange("p (j s) u -> p j s u", s=P),
            in_=back[:].rearrange("p j u s -> p j s u"),
        )

        quantise_wd(WD_SPLIT, N, wd_rest[:])
        y2_03 = second_product(EARLY_TILES)
        last2 = bank(3, [P, 2, UNIT])
        for which in range(2):
            product(last2[:, which, :], which, LAST_TILE, operands2[which])
        y1_2last = copy_out("y1_2last", last2[:, SUM, :], [P, UNIT])
        y2_04 = second_product(LAST_TILE)
        y1_21 = copy_out("y1_21", pair_product(SUM, 1, 4, operands2[SUM]), [P, 2, UNIT])
        y2_21 = pair_product(DIFFERENCE, 1, 5, operands2[DIFFERENCE])
        combine(3, DIFFERENCE, rounded1[3][DIFFERENCE][:])
        finish_tile(EARLY_TILES, (y1_03, y2_03))
        sums3 = quantise("unit30", rounded1[3][SUM][:], UNIT)
        y1_30 = copy_out("y1_30", pair_product(SUM, 0, 6, sums3), [P, 2, UNIT])
        y1_31 = copy_out("y1_31", pair_product(SUM, 1, 0, sums3), [P, 2, UNIT])
        last3 = [bank(index, [P, UNIT]) for index in (2, 4)]
        product(last3[SUM][:], SUM, LAST_TILE, sums3)
        y1_3last = copy_out("y1_3last", last3[SUM][:], [P, UNIT])
        finish_last(2, y1_2last, last2[:, DIFFERENCE, :])
        differences3 = quantise("unit31", rounded1[3][DIFFERENCE][:], UNIT)
        y2_30 = pair_product(DIFFERENCE, 0, 7, differences3)
        y2_31 = pair_product(DIFFERENCE, 1, 3, differences3)
        product(last3[DIFFERENCE][:], DIFFERENCE, LAST_TILE, differences3)

        finish_tile(LAST_TILE, (y1_04, y2_04))
        finish_pair(2, 1, y1_21, y2_21)
        finish_pair(3, 0, y1_30, y2_30)
        finish_pair(3, 1, y1_31, y2_31)
        finish_last(3, y1_3last, last3[DIFFERENCE][:])
